import numpy as np, ml_dtypes
CORES = [40,41,42,43,44,45,46,47]
N = 8
BF = ml_dtypes.bfloat16
def gentries(a):
    return np.ascontiguousarray(a.reshape(8, 16, -1).transpose(0, 2, 1)).reshape(8, -1)
def gtable(e):
    e = np.asarray(e); return np.ascontiguousarray(e.reshape(8, -1, 16).transpose(0, 2, 1)).reshape(128, -1).astype(np.int32)
V, R, L, T, M = 2048, 4096, 192, 10, 2048
def parts(rng):
    rec = rng.integers(0, 256, (N, 8, 16, R)); ch = rng.integers(0, R, (N, 8, 16, V)); at = rng.integers(0, 256, (N, 8, 16, L))
    key0 = np.where(rng.random((N, 8, L)) < 0.25, rng.integers(0, V // 16, (N, 8, L)), rng.integers(0, V, (N, 8, L)))
    th = rng.integers(1650, 2000, (N, 8, 1, 1)) + rng.integers(0, 250, (N, 8, 16, 1)); w = rng.integers(0, 16, (N, 8, 16, 1))
    return rec, ch, at, key0, th, w
def pack(rec, ch, at, key0, th, w):
    return {"rec": np.ascontiguousarray(rec.reshape(N, 128, R)).astype(np.float32).astype(BF), "ch": np.ascontiguousarray(ch.reshape(N, 128, V)).astype(np.int32),
            "at": np.ascontiguousarray(at.reshape(N, 128, L)).astype(np.float32).astype(BF), "key0": np.stack([gtable(a) for a in key0]),
            "th": np.ascontiguousarray(th.reshape(N, 128, 1)).astype(np.int32), "w": np.ascontiguousarray(w.reshape(N, 128, 1)).astype(np.int32)}
def setup_inputs(rng):
    return pack(*parts(rng))
def setup_inputs_clash(rng):
    rec, ch, at, key0, th, w = parts(rng); o = rng.permutation(L)
    at[..., o[1::2]] = at[..., o[0::2]]
    key0[:, 1::2] = rng.integers(0, V, (N, 4, 8))[np.arange(N)[:, None, None], np.arange(4)[None, :, None], rng.integers(0, 8, (N, 4, L))]
    key0[:, ::2, o[1::2]] = key0[:, ::2, o[0::2]]
    one = (np.arange(16)[None, None, :, None] == rng.integers(0, 16, (N, 8, 1, 1))).astype(np.int64)
    w = np.where((rng.random((N, 8, 1, 1)) < 0.5), one, w)
    w[rng.integers(0, N - 1), rng.integers(0, 8)] = 0
    ga, gb, gc = [int(i) for i in rng.permutation(8)[:3]]
    th[0, ga] = 4080; w[0, ga] = 0; th[1, ga] = 0
    for g in (gb, gc):
        key0[:, g] = np.argsort(rng.random((N, V)), axis=1)[:, :L]; th[0, g] = 0
    key0[:, gc, L - 1] = key0[:, gc, 0]
    return pack(rec, ch, at, key0, th, w)
def setup_inputs_ends(rng):
    rec, ch, at, key0, th, w = parts(rng)
    rec = 255 * (rng.random((N, 8, 16, R)) < rng.random((N, 8, 1, R))).astype(np.int64); at = 255 * (rng.random((N, 8, 16, L)) < rng.random((N, 8, 1, L))).astype(np.int64)
    at = np.where(rng.random((N, 8, 1, L)) < 0.3, 255 * rng.integers(0, 2, (N, 8, 1, L)), at)
    th = np.minimum(th + 700, 4080)
    key0[:, ::2] = rng.choice(np.array([0, 1, V - 2, V - 1]), (N, 4, L))
    ch[:, 4] = ch[:, 4, :1]
    for g in (3, 5):
        rec[:, g] = 255 * (rng.random((N, 1, R)) < 0.1); rec[:, g, :, R - 1458:R - 1455] = 0
        at[:, g] = 255 * (rng.random((N, 1, L)) < 0.9)
        ch[:, g] = rng.choice(np.array([0, R - 1, R - 1456, R - 1457, R - 1458]), (N, 16, V))
    th[:, 3] = 4079; th[:, 5] = rng.choice(np.array([0, 4079, 4080]), (N, 16, 1))
    w[:, 1] = 15
    rec[:, 1] = np.abs(255 * (rng.random((N, 16, R)) < 0.05) - rng.integers(0, 8, (N, 16, R)))
    at[:, 1] = np.abs(255 * (rng.random((N, 16, L)) < 0.6 + 0.4 * rng.random((N, 1, L))) - rng.integers(0, 8, (N, 16, L)))
    ch[:, 1, :, V - 1] = 0; rec[:, 1, :, 0] = 0; at[:, 1, :, 0] = 255; key0[:, 1, 0] = V - 1
    s = np.arange(N)[:, None] * L + np.argsort(rng.random((N, L)), axis=1) + 1
    turn = (np.arange(16)[None, :, None] + rng.integers(0, 16, (N, 1, L))) % 16
    at[:, 7] = s[:, None, :] // 16 + (turn < s[:, None, :] % 16); key0[:, 7] = s - 1
    rec[0, 7, :, :R - M] = 255; rec[0, 7, :, R - M:] = 0; ch[0, 7, 0] = R - M - 1
    th[0, 7] = 4080; th[0, 7, 0] = 2048; w[0, 7] = 0; w[0, 7, 0] = 1; th[1, 7] = 0
    return pack(rec, ch, at, key0, th, w)
def setup_inputs_quiet(rng):
    rec, ch, at, key0, th, w = parts(rng); q = rng.permutation(N)
    th[q[0]] = 4080; th[q[1]] = 0; th[:, rng.integers(0, 8)] = 4080; w[q[2]] = 15
    return pack(rec, ch, at, key0, th, w)
def setup_inputs_spread(rng):
    rec, ch, at, key0, th, w = parts(rng)
    rec = np.minimum((np.exp2(8 * rng.random((N, 8, 1, R))) * rng.random((N, 8, 16, R))).astype(np.int64), 255)
    at = np.minimum((np.exp2(8 * rng.random((N, 8, 1, L))) * rng.random((N, 8, 16, L))).astype(np.int64), 255)
    th = np.where(rng.random((N, 8, 16, 1)) < 0.1, rng.integers(0, 4081, (N, 8, 16, 1)), rng.integers(1200, 4081, (N, 8, 16, 1)))
    w = w * (rng.random((N, 8, 16, 1)) < 0.6)
    return pack(rec, ch, at, key0, th, w)
def setup_inputs_ties(rng):
    rec, ch, at, key0, th, w = parts(rng); u = rng.permutation(np.array([1, 1, 1, 2, 7, 16, 100, 255])).reshape(1, 8, 1, 1)
    rec = u * (rng.random((N, 8, 16, R)) < rng.random((N, 8, 1, R))); at = u * (rng.random((N, 8, 16, L)) < rng.random((N, 8, 1, L)))
    th = u * rng.integers(10, 15, (N, 8, 16, 1)) - rng.integers(0, 2, (N, 8, 16, 1))
    g = int(rng.integers(0, 8)); z = 255 * rng.integers(0, 2, 16); at[:, g] = z[:, None]
    th[:2, g] = 0; w[0, g] = 0
    e1, e2 = [R // 3 + int(i) for i in rng.integers(-150, 151, 2)]; steps = [e1, e2, R - e1 - e2]
    cs = [int(rng.integers(0, 100)), int(rng.integers(100, 200)), R - 1 - int(rng.integers(0, 100))]
    rec[1, g, :, 300] = z; ch[1, g, :, 0] = 300
    places = np.sort(rng.permutation(16)[:3])
    for i in range(3):
        far = int(np.nonzero(((37 * np.arange(M) + 1) & (M - 1)) == steps[i])[0][0])
        rec[1, g, :, cs[i]] = np.abs(z - (far // 16 + (np.arange(16) < far % 16)))
        rec[1, g, :, (cs[i] + steps[i]) % R] = z
        ch[1, g, places[i], 0] = cs[i]
    rec[0, g, 0, 1:] = 255 - z[0]; rec[0, g, :, 0] = z
    ch[0, g] = np.where(np.arange(V)[None, :] % 2 == 0, 0, rng.integers(1, R, (16, V)))
    key0[:, g] = 2 * rng.integers(0, V // 2, (N, L)); key0[2:N - 1, g] += 1; key0[1, g, 0] = 0
    return pack(rec, ch, at, key0, th, w)
def check_inputs(d):
    bad = []
    for k, hi in (("rec", 255), ("ch", R - 1), ("at", 255), ("key0", V - 1), ("th", 4080), ("w", 15)):
        v = np.asarray(d[k]).astype(np.float64)
        if not np.all((v >= 0) & (v <= hi) & (v == np.floor(v))): bad.append("range of " + k)
    return bad
def reference(rec, ch, at, key0, th, w):
    x = rec.astype(np.float32).astype(np.int32).reshape(N, 8, 16, R); a = at.astype(np.float32).astype(np.int32).reshape(N, 8, 16, L)
    c0 = ch.astype(np.int32).reshape(N, 8, 16, V); c = np.array(c0); lim = th.astype(np.int32).reshape(N, 8, 16, 1); wt = w.astype(np.int32).reshape(N, 8, 16, 1)
    k0 = np.stack([gentries(q) for q in key0]).astype(np.int64)
    key = np.array(k0); mark = np.zeros((N, 8, L), bool)
    low = np.tri(L, L, -1).astype(bool)
    for t in range(T):
        for b in range(N):
            r = (b + t) % N
            if t == 0 or r == 0:
                key[b] = k0[b]; mark[b] = False
            k = np.array(key[b]); m = np.array(mark[b])
            old = np.take_along_axis(c[r], k[:, None, :], 2)
            rows = np.take_along_axis(x[r], old.reshape(8, 1, 16 * L), 2).reshape(8, 16, 16, L)
            d = np.add.reduce(np.abs(rows - a[b][:, :, None, :]), axis=1)
            fail = d > lim[r]; bad = np.any(fail, axis=1); first = np.argmax(fail, axis=1)
            step = old + ((37 * d + 1) & (M - 1)); step = np.where(step >= R, step - R, step)
            mended = np.where(np.arange(16)[None, :, None] == first[:, None, :], step, old)
            back = np.take_along_axis(c0[r], k[:, None, :], 2)
            col = np.where(m[:, None, :], back, mended)
            want = m | bad
            lost = np.any((k[:, :, None] == k[:, None, :]) & want[:, None, :] & low[None], axis=2)
            win = want & ~lost
            for g in range(8):
                jj = np.nonzero(win[g])[0]
                c[r, g][:, k[g, jj]] = col[g][:, jj]
            mark[b] = m | win
            key[b] = np.add.reduce(wt[r] * d, axis=1) & (V - 1)
    end = [(r - (T - 1)) % N for r in range(N)]
    return {"yc": c.reshape(N, 128, V).astype(np.float32), "yk": np.stack([key[b] + V * mark[b] for b in end]).astype(np.float32)}

@@ -1,0 +1,405 @@
+from concourse.mybir import AluOpType, ActivationFunctionType
+
+NR, NT, L, V, R = 8, 10, 192, 2048, 4096
+SP = 48
+HL = 24
+CH = [48, 48, 36, 24, 12]
+MAGIC = 12582912.0
+ORDER = ("v0 s0 p0 v1 s1 p1 pl pre v2 s2 v3 s3 v4 s4 p24 keyf o2 r1 eq cc yc fl pc dm sgw pk qb py pu "
+         "pp rr ki mm kj ko fwd off yv ef val")
+
+BF, F32, F16, I32, U16 = "bfloat16", "float32", "float16", "int32", "uint16"
+SCRATCH = {name: ("sbuf", [128] + shape, dtype) for name, shape, dtype in [
+    ("chi", [V], I32), ("recs", [R + V], BF), ("tab", [SP + 2 * V], F32),
+    ("ats", [L], BF), ("ar", [NR * 16 * L], BF), ("df", [16 * L], BF), ("xh", [512], BF),
+    ("k0i", [12], I32), ("thi", [4], I32), ("wi", [4], I32), ("kb", [NT * 32], U16), ("ko", [NT * 16], U16),
+    ("mkb", [NT, 12, 16], BF), ("mko", [NT * L], BF),
+    ("jf", [V], F32), ("j16", [128], F32), ("rel", [288], BF), ("t1", [288], BF), ("t2", [288], BF), ("t3", [288], BF),
+    ("pi", [8], I32), ("col", [24], F32), ("eoi", [18], I32), ("eo", [18], U16), ("ao", [2], U16),
+    ("bm", [144], BF), ("bw", [144], F16), ("bo", [144], BF), ("b15", [128], BF), ("i1", [128], BF), ("im1", [128], BF),
+    ("i32", [128], F32), ("i37", [128], F16), ("im2", [128], BF), ("im8", [128], BF), ("ones", [128], BF),
+    ("lz", [128], BF), ("s8f", [8], F32), ("s8b", [8], BF), ("jrow", [L], BF), ("cpat", [288], BF),
+    ("cand", [L], U16), ("keyf", [16], F32), ("krow", [288], F32), ("eq", [288], BF), ("pp", [288], BF),
+    ("rr", [288], BF), ("mm", [16], F32), ("off", [12], U16), ("o2f", [12], F32), ("o2", [12], U16),
+    ("r1", [L], F32), ("c1", [L], F32), ("sgw", [L], BF), ("yv", [L], F32), ("ef", [L], F32), ("val", [L], F32),
+    ("dm", [L], F16), ("fl", [12, 16], BF), ("qb", [L], BF), ("wn", [L], BF), ("ki", [12], I32), ("kj", [12], I32),
+    ("ro", [V], F32), ("so", [V], BF), ("oc", [V], F32), ("yks", [L], F32)]}
+PSUM = ("pd", "pk", "pc", "pu", "py", "pv", "pm")
+for _b in PSUM:
+    SCRATCH[_b] = ("psum", [128, 1024 if _b == "pc" else 512], F32)
+SEMAPHORES = (["qv", "qs", "qp", "qg", "sent", "lsm", "lch", "lrec", "lext", "lk0", "lat", "stored"]
+              + ["ka%d" % t for t in range(NT)] + ["ma%d" % t for t in range(NT)]
+              + ["aa%d" % h for h in range(NR)] + ["ab%d" % h for h in range(NR)])
+
+A = AluOpType
+F = ActivationFunctionType
+
+
+def rank_program(g, core, T, topo):
+    rank = T.rank_of(core)
+    if rank is None:
+        return
+    eng = {"v": g.vector, "s": g.scalar, "p": g.tensor, "g": g, "y": g.sync}
+    qsem = {"v": "qv", "s": "qs", "p": "qp", "g": "qg"}
+    count = {}
+    know = {q: {} for q in eng}
+    snap = {}
+    wrote, read = {}, {}
+
+    def need(q, ev):
+        sem, n = ev
+        if know[q].get(sem, 0) >= n:
+            return
+        eng[q].wait_ge(T.sem[sem], n)
+        know[q][sem] = n
+        for s, m in snap.get(ev, {}).items():
+            if know[q].get(s, 0) < m:
+                know[q][s] = m
+
+    def order(q, rd, wr):
+        evs = {}
+        for b in list(rd) + list(wr):
+            if b in wrote and not (q == "p" and wrote[b][0] == "qp"):
+                evs[wrote[b][0]] = max(evs.get(wrote[b][0], 0), wrote[b][1])
+        for b in wr:
+            for s, n in read.get(b, {}).items():
+                if not (q == "p" and s == "qp"):
+                    evs[s] = max(evs.get(s, 0), n)
+        for ev in sorted(evs.items(), key=lambda e: e[0] == qsem.get(q)):
+            need(q, ev)
+
+    def note(ev, q, rd, wr):
+        snap[ev] = dict(know[q])
+        for b in rd:
+            read.setdefault(b, {})[ev[0]] = ev[1]
+        for b in wr:
+            wrote[b] = ev
+            read[b] = {}
+
+    def op(q, rd, wr, call):
+        wr = list(wr) + [b for b in rd if b in PSUM]
+        rd = [b for b in rd if b not in PSUM]
+        order(q, rd, wr)
+        sem = qsem[q]
+        count[sem] = count.get(sem, 0) + 1
+        call(eng[q]).then_inc(T.sem[sem], 1)
+        note((sem, count[sem]), q, rd, wr)
+
+    def dma(q, sem, rd, wr, out, in_, **kw):
+        order(q, rd, wr)
+        count[sem] = count.get(sem, 0) + 16
+        eng[q].dma_start(out, in_, **kw).then_inc(T.sem[sem], 16)
+        note((sem, count[sem]), q, rd, wr)
+
+    def send(to, sem, rd, out, in_):
+        order("g", rd, [])
+        dst = T.cores[to]
+        rid, pid, _ = topo.addr(dst)
+        g.remote_dma(out, in_, T.sem[sem], T.sem.sent, pid, rid, topo.mask(core, dst))
+        count["sent"] = count.get("sent", 0) + len(topo.engines(core, dst))
+
+    def lands(frm, sem, region):
+        count[sem] = len(topo.engines(T.cores[frm], core))
+        wrote[region] = (sem, count[sem])
+
+    def ts(out, in0, s1, s2, o0, o1, rd, wr):
+        if o1 is None:
+            op("v", rd, wr, lambda e: e.tensor_scalar(out, in0, s1, None, o0))
+        else:
+            op("v", rd, wr, lambda e: e.tensor_scalar(out, in0, s1, s2, o0, o1))
+
+    def tt(out, a, b, o, rd, wr):
+        op("v", rd, wr, lambda e: e.tensor_tensor(out, a, b, o))
+
+    def cp(out, in_, rd, wr):
+        op("v", rd, wr, lambda e: e.tensor_copy(out, in_))
+
+    def act(out, in_, f, rd, wr, **kw):
+        op("s", rd, wr, lambda e: e.activation(out, in_, f, **kw))
+
+    def mm(bank, out, terms, first=True, final=True):
+        for n, (lt, rhs, rd) in enumerate(terms):
+            op("p", rd, [bank],
+               lambda e: e.matmul(out, lt, rhs, first and n == 0, final and n == len(terms) - 1))
+
+    def iota(out, pat, base, mul, wr, flt):
+        if flt:
+            op("g", [], wr, lambda e: e.iota(out, pat, base, mul, allow_small_or_imprecise_dtypes=True))
+        else:
+            op("g", [], wr, lambda e: e.iota(out, pat, base, mul))
+
+    nxt, prv = (rank + 1) % NR, (rank - 1) % NR
+    W = 16 * L
+
+    def forward(h, k, rd):
+        half = T.ar[:, h * W + k * W // 2:h * W + (k + 1) * W // 2]
+        send(nxt, "a%s%d" % ("ab"[k], h), rd, half, half)
+
+    for s in range(1, NR):
+        for k in "ab":
+            lands(prv, "a%s%d" % (k, (rank - s) % NR), "r%s%d" % (k, (rank - s) % NR))
+    if rank == 0:
+        for t in range(1, NR):
+            lands((-t) % NR, "ka%d" % t, "kb%d" % t)
+    else:
+        for t in range(1, NT):
+            lands(prv, "ka%d" % t, "kb%d" % t)
+            lands(prv, "ma%d" % t, "mk%d" % t)
+
+    dma("s", "lat", [], ["ats"], T.ats[:], T.at[:])
+    dma("s", "lk0", [], ["k0i"], T.k0i[:], T.key0[:])
+    dma("y", "lch", [], ["chi"], T.chi[:], T.ch[:])
+    dma("y", "lrec", [], ["recs"], T.recs[:, 0:R], T.rec[:])
+    iota(T.pi[:, 0:1], [[0, 1]], 0, 1, ["pi0"], False)
+    iota(T.jf[:, 0:192], [[1, 192]], 0, 0, ["jfa"], True)
+    iota(T.j16[:], [[16, 8], [0, 16]], 0, 0, ["j16"], True)
+    dma("g", "lsm", [], ["thi"], T.thi[:, 0:1], T.th[:], allow_slow_non_contiguous=True)
+    dma("g", "lsm", [], ["wi"], T.wi[:, 0:1], T.w[:], allow_slow_non_contiguous=True)
+    wrote["thi"] = wrote["wi"]
+    iota(T.rel[:, 0:192], [[0, 6], [1, 32]], -16, 0, ["rela"], True)
+    iota(T.rel[:, 192:288], [[0, 6], [1, 16]], 0, 0, ["relb"], True)
+    iota(T.eoi[:, 0:12], [[2, 6], [0, 2]], 1, 0, ["eoia"], False)
+    iota(T.eoi[:, 12:18], [[2, 6]], 0, 0, ["eoib"], False)
+    iota(T.jf[:, 192:V], [[1, V - 192]], 192, 0, ["jfb"], True)
+
+    def c(k):
+        return T.col[:, k:k + 1]
+    P, GB, U, OD, G15, U1, SC, SI, SB, D0, D1, TH, WT, X0, X1, X2, X3 = range(17)
+    j = T.jf[:, 0:128]
+    ts(T.pi[:, 1:2], T.pi[:, 0:1], 112, None, A.bitwise_and, None, ["pi0"], ["pi1"])
+    ts(T.pi[:, 2:3], T.pi[:, 0:1], 15, None, A.bitwise_and, None, ["pi0"], ["pi2"])
+    ts(T.pi[:, 3:4], T.pi[:, 0:1], 1, None, A.bitwise_and, None, ["pi0"], ["pi3"])
+    op("v", [], ["keyf"], lambda e: e.memset(T.keyf[:], 0.0))
+    op("v", [], ["spare"], lambda e: e.memset(T.tab[:, 0:SP], 0.0))
+    cp(T.col[:, 0:4], T.pi[:, 0:4], ["pi0", "pi1", "pi2", "pi3"], ["c0"])
+    ts(c(G15), c(GB), 15.0, None, A.add, None, ["c0"], ["g15"])
+    ts(c(U1), c(U), 1.0, None, A.add, None, ["c0"], ["u1"])
+    ts(c(X0), c(U), 15.0, 4095.0, A.is_equal, A.mult, ["c0"], ["x0"])
+    ts(c(X1), c(U), 8.0, -192.0, A.mult, A.add, ["c0"], ["x1"])
+    ts(c(D0), c(U), 16.0, None, A.add, None, ["c0"], ["d0"])
+    ts(c(D1), c(U), 32.0, None, A.add, None, ["c0"], ["d1"])
+    ts(T.bm[:], T.jf[:, 0:144], c(G15), None, A.is_equal, None, ["jfa", "g15"], ["bm"])
+    ts(c(SI), c(X0), 1.0, None, A.add, None, ["x0"], ["si"])
+    ts(c(SC), c(X0), -1.0 / 4096, 1.0, A.mult, A.add, ["x0"], ["sc"])
+    ts(c(X2), c(X1), c(OD), None, A.mult, None, ["x1", "c0"], ["x2"])
+    ts(c(SB), c(SC), float(SP), None, A.mult, None, ["sc"], ["sb"])
+    ts(c(X3), c(X2), c(X1), 399.0, A.add, A.add, ["x2", "x1"], ["x3"])
+    ts(T.i1[:], j, c(P), None, A.is_equal, None, ["jfa", "c0"], ["i1"])
+    ts(T.ao[:, 0:1], c(X3), 287.0, None, A.min, None, ["x3"], ["ao"])
+
+    for i in range(16):
+        o = T.ar[:, rank * W + i:(rank + 1) * W:16]
+        if i % 2 == 1:
+            act(o, T.ats[:], F.Copy, ["ats"], ["own%d" % i])
+        else:
+            cp(o, T.ats[:], ["ats"], ["own%d" % i])
+    own = ["own%d" % i for i in range(16)]
+
+    ts(T.t1[:], T.rel[:], c(U), -2.0, A.is_equal, A.mult, ["rela", "relb", "c0"], ["t1"])
+    act(T.t3[:], T.t1[:], F.Identity, ["t1"], ["t3"], bias=1.0)
+    for out, src, f, nm in ((T.im1[:], T.i1[:], -1.0, "im1"), (T.i32[:], T.i1[:], 1.0, "i32"),
+                            (T.im2[:], T.i1[:], -2048.0, "im2"), (T.im8[:], T.i1[:], -8192.0, "im8"),
+                            (T.s8f[:], T.i1[:, 0:128:16], 1.0, "s8f"), (T.s8b[:], T.i1[:, 0:128:16], 2048.0, "s8b"),
+                            (T.bo[:], T.bm[:], 128.0, "bo"), (T.b15[:], T.bm[:, 0:128], 128.0 / 4096, "b15"),
+                            (T.jrow[:], T.jf[:, 0:L], 1.0 / 2048, "jrow")):
+        act(out, src, F.Identity, ["i1", "bm", "jfa"], [nm], scale=f)
+    ts(T.t2[:], T.rel[:], c(U1), 4096.0, A.is_equal, A.mult, ["rela", "relb", "u1"], ["t2"])
+    ts(T.i37[:], j, c(P), 37.0, A.is_equal, A.mult, ["jfa", "c0"], ["i37"])
+    ts(T.ones[:], T.j16[:], c(GB), None, A.is_equal, None, ["j16", "c0"], ["ones"])
+    ts(T.qb[:, 0:128], j, c(P), -8192.0, A.is_gt, A.mult, ["jfa", "c0"], ["qb"])
+    ts(T.wn[:, 0:128], j, c(P), 4096.0, A.is_equal, A.mult, ["jfa", "c0"], ["wn"])
+    cp(T.eo[:], T.eoi[:], ["eoia", "eoib"], ["eo"])
+    tt(T.qb[:, 0:128], T.qb[:, 0:128], T.wn[:, 0:128], A.add, ["qb", "wn"], ["qb"])
+    tt(T.cpat[:], T.t3[:], T.t2[:], A.add, ["t3", "t2"], ["cpat"])
+    tt(T.lz[:], T.qb[:, 0:128], T.ones[:], A.mult, ["qb", "ones"], ["lz"])
+    op("v", [], ["cpat"], lambda e: e.memset(T.cpat[:, 0:192:32], 0.0))
+    op("v", [], ["cpat"], lambda e: e.memset(T.cpat[:, 192:288:16], 0.0))
+
+    cp(T.kb[:, 0:12], T.k0i[:], ["k0i"], ["kb0"])
+    if rank != 0:
+        t0 = (-rank) % NR
+        send(0, "ka%d" % t0, ["kb0"], T.kb[:, 32 * t0:32 * t0 + 12], T.kb[:, 0:12])
+
+    tabw = T.tab[:, SP:SP + V]
+    lo = [HL + sum(CH[:k]) for k in range(len(CH) + 1)]
+
+    def marks(t, fresh, kl, kbn, mo):
+        if fresh:
+            tt(mo, tabw.indirect(kl), T.val[:], A.is_equal, ["tab", kbn, "val"], ["mo%d" % t])
+        else:
+            tt(T.wn[:], tabw.indirect(kl), T.val[:], A.is_equal, ["tab", kbn, "val"], ["wn"])
+            mm("pm", T.pm[:, 0:L], [(T.i1[:], T.mkb[:, t], ["i1", "mk%d" % t]), (T.i1[:], T.wn[:], ["i1", "wn"])])
+            act(mo, T.pm[:, 0:L], F.Sign, ["pm"], ["mo%d" % t])
+
+    for t in range(NT):
+        home = (rank - t) % NR
+        fresh = t == 0 or rank == 0
+        last = t == NT - 1
+        hand_on = last or rank != NR - 1
+        kt = t % NR if rank == 0 else t
+        kl, kbn, mkn = T.kb[:, 32 * kt:32 * kt + 12], "kb%d" % kt, "mk%d" % t
+        arn = own if home == rank else ["ra%d" % home, "rb%d" % home]
+        mo = T.mko[:, L * t:L * t + L]
+        ahead = (rank - t - 1) % NR
+
+        if t == 0:
+            cp(T.cand[:], T.chi[:, 0:V].indirect(kl), ["chi", kbn], ["cand"])
+        else:
+            cp(T.cand[:], tabw.indirect(kl), ["tab", kbn], ["cand"])
+        if kt == t:
+            cp(T.kb[:, 32 * kt + 12:32 * kt + 18], T.kb[:, 32 * kt:32 * kt + 12:2], [kbn], [kbn + "e"])
+        if t == 0:
+            H = V // 2
+            for h in range(2):
+                cp(T.tab[:, SP + V + h * H:SP + V + (h + 1) * H], T.chi[:, h * H:(h + 1) * H], ["chi"], ["ch0%d" % h])
+                act(T.tab[:, SP + h * H:SP + (h + 1) * H], T.tab[:, SP + V + h * H:SP + V + (h + 1) * H], F.Copy,
+                    ["ch0%d" % h], ["tab%d" % h])
+            wrote["tab"], wrote["ch0"] = wrote["tab1"], wrote["ch01"]
+            order("g", ["recs"], [])
+            forward(rank, 0, own)
+            forward(rank, 1, own)
+            dma("y", "lext", ["recs"], ["rece"], T.recs[:, R:R + V], T.rec[:, 0:V])
+
+        recw = T.recs[:, 0:R] if t == 0 else T.recs[:, 0:R + V]
+        recn = ["recs"] if t == 0 else ["recs", "rece"]
+        tag = (L * t - (960 if t < 5 else 959)) / 2048.0
+
+        act(T.xh[:, 0:16 * HL], recw.indirect(T.cand[:, 0:HL]), F.Copy, recn + ["cand"], ["xh"])
+        mm("pv", T.pv[:, 0:16 * HL], [(T.i1[:], T.xh[:, 0:16 * HL], ["i1", "xh"]),
+                                      (T.im1[:], T.ar[:, home * W:home * W + 16 * HL], ["im1"] + arn)])
+        act(T.krow[:], T.jf[:, 0:V].indirect(T.kb[:, 32 * kt:32 * kt + 18]), F.Identity,
+            ["jfa", "jfb", kbn, kbn + "e", "sc", "sb"], ["krow"], bias=c(SB), scale=c(SC))
+        act(T.df[:, 0:16 * HL], T.pv[:, 0:16 * HL], F.Abs, ["pv"], ["dfh"])
+
+        def step(nm):
+            if nm[0] in "vsp" and nm[1:].isdigit():
+                k, k2 = int(nm[1]), int(nm[-1])
+                a, b = lo[k], lo[k2 + 1]
+                if nm[0] == "v":
+                    tt(T.df[:, 16 * a:16 * b], recw.indirect(T.cand[:, a:b]),
+                       T.ar[:, home * W + 16 * a:home * W + 16 * b], A.subtract, recn + ["cand"] + arn, ["df%d" % k])
+                elif nm[0] == "s":
+                    act(T.df[:, 16 * a:16 * b], T.df[:, 16 * a:16 * b], F.Abs, [], ["df%d" % k])
+                else:
+                    a = 0 if k == 0 else a
+                    rd = ["bm"] + ["df%d" % q for q in range(k, k2 + 1)] + (["dfh"] if k == 0 else [])
+                    mm("pd", T.pd[:, a:b], [(T.bm[:, 15 - i:143 - i], T.df[:, 16 * a + i:16 * b:16], rd)
+                                            for i in range(16)])
+            elif nm == "pl":
+                if not fresh:
+                    mm("pm", T.pm[:, 0:12], [(T.bo[:, 15 - u:143 - u] if u < 15 else T.b15[:], T.mkb[:, t, :, u],
+                                              ["bo", "b15", mkn]) for u in range(16)])
+            elif nm == "pre":
+                mm("py", T.py[:, 0:L], [(T.i1[:], T.jrow[:], ["i1", "jrow"])], True, False)
+                if not fresh:
+                    mm("pc", T.pc[:, 320:512], [(T.i1[:], T.mkb[:, t], ["i1", mkn])], True, False)
+                    mm("pc", T.pc[:, 512:608], [(T.i1[:], T.mkb[:, t, 0:12:2, :], ["i1", mkn])], True, False)
+                    mm("pu", T.pu[:, 0:L], [(T.im8[:], T.mkb[:, t], ["im8", mkn])], True, False)
+            elif nm == "keyf":
+                ts(T.keyf[:, 0:12], kl, float(SP), c(SC), A.add, A.mult, [kbn, "sc"], ["keyf"])
+                if t == 0:
+                    cp(c(TH), T.thi[:, 0:1], ["thi"], ["th"])
+                    cp(c(WT), T.wi[:, 0:1], ["wi"], ["wt"])
+                    ts(T.bw[:], T.jf[:, 0:144], c(G15), c(WT), A.is_equal, A.mult, ["jfa", "g15", "wt"], ["bw"])
+            elif nm == "o2":
+                if not fresh:
+                    tt(T.o2f[:], T.pm[:, 0:12], T.keyf[:, 0:12], A.add, ["pm", "keyf"], ["o2f"])
+                    ts(T.o2[:], T.o2f[:], c(SI), -float(SP), A.mult, A.add, ["o2f", "si"], ["o2"])
+            elif nm == "r1":
+                if fresh:
+                    act(T.r1[:], tabw.indirect(kl), F.Identity, ["tab", kbn], ["r1"], bias=MAGIC)
+                else:
+                    act(T.r1[:], T.tab[:, SP:SP + 2 * V].indirect(T.o2[:]), F.Identity, ["tab", "ch0", "o2"], ["r1"],
+                        bias=MAGIC)
+            elif nm == "eq":
+                tt(T.eq[:], T.keyf[:, 0:16].indirect(T.eo[:]), T.krow[:], A.is_equal, ["keyf", "eo", "krow"], ["eq"])
+            elif nm == "cc":
+                act(T.c1[:], T.r1[:], F.Identity, ["r1"], ["c1"], bias=-MAGIC)
+            elif nm == "sgw":
+                act(T.sgw[:], T.c1[:], F.Sign, ["c1"], ["sgw"], bias=-4095.5)
+            elif nm == "yc":
+                mm("py", T.py[:, 0:L], [(T.i32[:], T.c1[:], ["i32", "c1"])], False, False)
+            elif nm == "py":
+                mm("py", T.py[:, 0:L], [(T.im2[:], T.sgw[:], ["im2", "sgw"])], False, True)
+            elif nm == "yv":
+                act(T.yv[:], T.py[:, 0:L], F.Identity, ["py"], ["yv"], bias=-2048.0 + tag)
+            elif nm == "fl":
+                ts(T.fl[:], T.pd[:, 0:L], c(TH), None, A.is_gt, None, ["pd", "th"], ["fl"])
+            elif nm == "dm":
+                ts(T.dm[:], T.pd[:, 0:L], -2048.0, None, A.add, None, ["pd"], ["dm"])
+            elif nm == "qb":
+                act(T.qb[:], T.pd[:, 0:L], F.Identity, ["pd"], ["qb"], scale=37.0 / 2048, bias=155.0 - 1022.5 / 2048)
+            elif nm == "pc":
+                mm("pc", T.pc[:, 320:512], [(T.ones[:], T.fl[:], ["ones", "fl"])], fresh, True)
+                mm("pc", T.pc[:, 512:608], [(T.ones[:], T.fl[:, 0:12:2, :], ["ones", "fl"])], fresh, True)
+            elif nm == "pu":
+                mm("pu", T.pu[:, 0:L], [(T.lz[:], T.fl[:], ["lz", "fl"]), (T.i37[:], T.dm[:], ["i37", "dm"]),
+                                        (T.im2[:], T.qb[:], ["im2", "qb"])], fresh, True)
+            elif nm == "ef":
+                act(T.ef[:], T.pu[:, 0:L], F.Relu, ["pu"], ["ef"], bias=float(1 + 2048 * 192 - 4096))
+            elif nm == "pp":
+                tt(T.pp[:], T.pc[:, 320:608], T.eq[:], A.min, ["pc", "eq"], ["pp"])
+            elif nm == "rr":
+                op("v", ["cpat", "pp"], ["rr"],
+                   lambda e: e.tensor_tensor_scan(T.rr[:], T.cpat[:], T.pp[:], 0.0, A.mult, A.add))
+            elif nm == "mm":
+                tt(T.mm[:], T.rr[:, 0:288].indirect(T.ao[:, 0:1]), T.keyf[:], A.min, ["rr", "ao", "keyf"], ["mm"])
+            elif nm == "off":
+                ts(T.off[:, 0:12:2], T.mm[:, 0:12:2], c(SI), c(D0), A.mult, A.max, ["mm", "si", "d0"], ["off0"])
+                ts(T.off[:, 1:12:2], T.mm[:, 1:12:2], c(SI), c(D1), A.mult, A.max, ["mm", "si", "d1"], ["off1"])
+            elif nm == "fwd":
+                if t < NR - 2:
+                    forward(ahead, 0, ["ra%d" % ahead])
+            elif not hand_on:
+                pass
+            elif nm == "pk":
+                mm("pk", T.pk[:, 0:12], [(T.bw[:, 15 - u:143 - u], T.dm[:, u:L:16], ["bw", "dm"]) for u in range(16)])
+            elif nm == "ki":
+                cp(T.ki[:], T.pk[:, 0:12], ["pk"], ["ki"])
+            elif nm == "kj":
+                ts(T.kj[:], T.ki[:], V - 1, None, A.bitwise_and, None, ["ki"], ["kj"])
+            elif nm == "ko":
+                cp(T.ko[:, 16 * t:16 * t + 12], T.kj[:], ["kj"], ["ko%d" % t])
+                if not last:
+                    send(nxt, "ka%d" % (t + 1), ["ko%d" % t], T.kb[:, 32 * (t + 1):32 * (t + 1) + 12],
+                         T.ko[:, 16 * t:16 * t + 12])
+            elif nm == "val":
+                mm("pv", T.pv[:, 0:L], [(T.i32[:], T.yv[:], ["i32", "yv"]), (T.i32[:], T.ef[:], ["i32", "ef"])])
+                act(T.val[:], T.pv[:, 0:L], F.Copy, ["pv"], ["val"])
+        for nm in ORDER.split():
+            step(nm)
+
+        for p in range(5, -1, -1):
+            tt(T.tab[:, 0:SP + V].indirect(T.off[:, 2 * p:2 * p + 2]), T.yv[:, 32 * p:32 * p + 32],
+               T.ef[:, 32 * p:32 * p + 32], A.add, ["off0", "off1", "yv", "ef"], ["tab", "spare"])
+        if hand_on and not last:
+            marks(t, fresh, kl, kbn, mo)
+            send(nxt, "ma%d" % (t + 1), ["mo%d" % t], T.mkb[:, t + 1], mo)
+        if t < NR - 2:
+            forward(ahead, 1, ["rb%d" % ahead])
+
+    t = NT - 1
+    banks = ["pu", "py", "pc", "pd", "pv"]
+    cut = [0, 256, 768, 1280, 1792, 2048]
+    for k in range(5):
+        a, b = cut[k], cut[k + 1]
+        act(T.so[:, a:b], T.tab[:, SP + a:SP + b], F.Sign, ["tab"], ["so%d" % k], bias=-4095.5)
+        mm(banks[k], T[banks[k]][:, 0:b - a], [(T.im2[:], T.so[:, a:b], ["im2", "so%d" % k])])
+    for k in range(6):
+        if k < 5:
+            a, b = cut[k], cut[k + 1]
+            ts(T.ro[:, a:b], T.tab[:, SP + a:SP + b], MAGIC, -(MAGIC + 2048.0), A.add, A.add, ["tab"], ["ro%d" % k])
+        if k > 0:
+            a, b = cut[k - 1], cut[k]
+            tt(T.oc[:, a:b], T[banks[k - 1]][:, 0:b - a], T.ro[:, a:b], A.add, [banks[k - 1], "ro%d" % (k - 1)],
+               ["oc%d" % k])
+            dma("y", "stored", ["oc%d" % k], [], T.yc[:, a:b], T.oc[:, a:b])
+        if k == 2:
+            marks(t, fresh, kl, kbn, mo)
+    act(T.krow[:, 0:L], T.jf[:, 0:V].indirect(T.ko[:, 16 * t:16 * t + 12]), F.Identity,
+        ["jfa", "jfb", "ko%d" % t], ["krow"])
+    mm("pk", T.pk[0:8, 0:L], [(T.s8f[:], T.krow[:, 0:L], ["s8f", "krow"]), (T.s8b[:], mo, ["s8b", "mo%d" % t])])
+    act(T.yks[0:8, :], T.pk[0:8, 0:L], F.Copy, ["pk"], ["yks"])
+    dma("s", "stored", ["yks"], [], T.yk[:], T.yks[0:8, :])
+    for sem, n in count.items():
+        g.wait_ge(T.sem[sem], n)

@@ -1,34 +1,39 @@
 from concourse.mybir import AluOpType, ActivationFunctionType
 
 NR, NT, L, V, R = 8, 10, 192, 2048, 4096
-SP = 48
-HL = 24
-CH = [48, 48, 36, 24, 12]
+SP = 32
+CUT = [0, 32, 64, 96, 128, 160, 180, 192]
+DCUT = [0, 64, 128, 192]
+NA = 128
 MAGIC = 12582912.0
-ORDER = ("v0 s0 p0 v1 s1 p1 pl pre v2 s2 v3 s3 v4 s4 p24 keyf o2 r1 eq cc yc fl pc dm sgw pk qb py pu "
-         "pp rr ki mm kj ko fwd off yv ef val")
+ORDER = ("candA <wn <pm xh v1 <mo pv v2 v3 s1 candZ kex keyf wf s0 v4 v6 s2 d0 s3 py krow eq s4 s6 d1 flA dmA pl o2 "
+         "v5 pcA qbA pkA puA rrA r1 kiA offA s5 d2 c1 kjA preZ yv efA koA sc0 flZ pcZ dmZ qbZ puZ efZ sc1 pkZ rrZ "
+         "sc2 offZ sc3 kiZ sc4 kjZ sc5 koZ")
 
 BF, F32, F16, I32, U16 = "bfloat16", "float32", "float16", "int32", "uint16"
 SCRATCH = {name: ("sbuf", [128] + shape, dtype) for name, shape, dtype in [
-    ("chi", [V], I32), ("recs", [R + V], BF), ("tab", [SP + 2 * V], F32),
-    ("ats", [L], BF), ("ar", [NR * 16 * L], BF), ("df", [16 * L], BF), ("xh", [512], BF),
-    ("k0i", [12], I32), ("thi", [4], I32), ("wi", [4], I32), ("kb", [NT * 32], U16), ("ko", [NT * 16], U16),
-    ("mkb", [NT, 12, 16], BF), ("mko", [NT * L], BF),
-    ("jf", [V], F32), ("j16", [128], F32), ("rel", [288], BF), ("t1", [288], BF), ("t2", [288], BF), ("t3", [288], BF),
-    ("pi", [8], I32), ("col", [24], F32), ("eoi", [18], I32), ("eo", [18], U16), ("ao", [2], U16),
-    ("bm", [144], BF), ("bw", [144], F16), ("bo", [144], BF), ("b15", [128], BF), ("i1", [128], BF), ("im1", [128], BF),
-    ("i32", [128], F32), ("i37", [128], F16), ("im2", [128], BF), ("im8", [128], BF), ("ones", [128], BF),
-    ("lz", [128], BF), ("s8f", [8], F32), ("s8b", [8], BF), ("jrow", [L], BF), ("cpat", [288], BF),
-    ("cand", [L], U16), ("keyf", [16], F32), ("krow", [288], F32), ("eq", [288], BF), ("pp", [288], BF),
-    ("rr", [288], BF), ("mm", [16], F32), ("off", [12], U16), ("o2f", [12], F32), ("o2", [12], U16),
-    ("r1", [L], F32), ("c1", [L], F32), ("sgw", [L], BF), ("yv", [L], F32), ("ef", [L], F32), ("val", [L], F32),
-    ("dm", [L], F16), ("fl", [12, 16], BF), ("qb", [L], BF), ("wn", [L], BF), ("ki", [12], I32), ("kj", [12], I32),
+    ("chi", [V], I32), ("recs", [2 * R], BF), ("tab", [SP + 2 * V], F32),
+    ("ats", [L], BF), ("atr", [L], BF), ("ar", [NR * 16 * L], BF), ("df", [16 * L], BF), ("xh", [512], BF),
+    ("k0i", [12], I32), ("k0h", [12], F16), ("thi", [4], I32), ("wi", [4], I32),
+    ("kb", [NT * 32], U16), ("ko", [NT * 16], U16), ("mkb", [NT, 6, 32], BF), ("mko", [NT * L], BF),
+    ("jf", [V], F32), ("j16", [128], F32), ("rel", [1, 50], BF), ("t1", [50], BF), ("t2", [50], BF),
+    ("pi", [8], I32), ("col", [24], F32), ("eoi", [18], I32), ("eo", [18], U16), ("rvf", [12], F32), ("rv", [12], U16),
+    ("bm", [144], BF), ("bw", [144], F16), ("bo", [144], BF), ("i1", [128], BF), ("im1", [128], BF),
+    ("in2", [128], BF), ("i64", [128], BF), ("i32", [128], F32), ("i16", [128], F16), ("i37", [128], F16),
+    ("im2", [128], BF), ("im4", [128], BF), ("im8", [128], BF), ("ones", [128], BF), ("on2", [128], BF),
+    ("lz", [128], BF), ("prv", [128], F16), ("s8f", [8], F32), ("s8b", [8], BF),
+    ("tags", [NT * L], F16), ("dpat", [1, 50], BF),
+    ("cand", [L], U16), ("keyf", [16], F32), ("krow", [288], F32), ("ne", [288], BF), ("zero", [300], BF),
+    ("rr", [6, 50], F32),
+    ("off", [12], U16), ("o2", [12], U16), ("r1", [L], F32), ("c1", [L], F32), ("wf", [L], BF), ("yv", [L], F32),
+    ("ef", [L], F32), ("dm", [L], F16), ("fl", [6, 32], BF), ("qb", [L], BF), ("wn", [L], BF),
+    ("ki", [12], I32), ("kj", [12], I32),
     ("ro", [V], F32), ("so", [V], BF), ("oc", [V], F32), ("yks", [L], F32)]}
-PSUM = ("pd", "pk", "pc", "pu", "py", "pv", "pm")
+PSUM = ("b0", "b1", "b2", "b3", "b4", "b5", "b6", "b7")
 for _b in PSUM:
-    SCRATCH[_b] = ("psum", [128, 1024 if _b == "pc" else 512], F32)
-SEMAPHORES = (["qv", "qs", "qp", "qg", "sent", "lsm", "lch", "lrec", "lext", "lk0", "lat", "stored"]
-              + ["ka%d" % t for t in range(NT)] + ["ma%d" % t for t in range(NT)]
+    SCRATCH[_b] = ("psum", [128, 8, 64] if _b in ("b3", "b4") else [128, 512], F32)
+SEMAPHORES = (["qv", "qs", "qp", "qg", "sent", "lsm", "lch", "lrec", "lext", "lex2", "lk0", "lat", "stored"]
+              + ["k%s%d" % (z, t) for t in range(NT) for z in "AZ"] + ["ma%d" % t for t in range(NT)]
               + ["aa%d" % h for h in range(NR)] + ["ab%d" % h for h in range(NR)])
 
 A = AluOpType
@@ -58,13 +63,15 @@ def rank_program(g, core, T, topo):
 
     def order(q, rd, wr):
         evs = {}
-        for b in list(rd) + list(wr):
-            if b in wrote and not (q == "p" and wrote[b][0] == "qp"):
+        for b in rd:
+            if b in wrote:
                 evs[wrote[b][0]] = max(evs.get(wrote[b][0], 0), wrote[b][1])
         for b in wr:
+            free = qsem.get(q) if b in PSUM else None
+            if b in wrote and wrote[b][0] != free:
+                evs[wrote[b][0]] = max(evs.get(wrote[b][0], 0), wrote[b][1])
             for s, n in read.get(b, {}).items():
-                if not (q == "p" and s == "qp"):
-                    evs[s] = max(evs.get(s, 0), n)
+                evs[s] = max(evs.get(s, 0), n)
         for ev in sorted(evs.items(), key=lambda e: e[0] == qsem.get(q)):
             need(q, ev)
 
@@ -98,9 +105,10 @@ def rank_program(g, core, T, topo):
         g.remote_dma(out, in_, T.sem[sem], T.sem.sent, pid, rid, topo.mask(core, dst))
         count["sent"] = count.get("sent", 0) + len(topo.engines(core, dst))
 
-    def lands(frm, sem, region):
+    def lands(frm, sem, *regions):
         count[sem] = len(topo.engines(T.cores[frm], core))
-        wrote[region] = (sem, count[sem])
+        for b in regions:
+            wrote[b] = (sem, count[sem])
 
     def ts(out, in0, s1, s2, o0, o1, rd, wr):
         if o1 is None:
@@ -114,11 +122,14 @@ def rank_program(g, core, T, topo):
     def cp(out, in_, rd, wr):
         op("v", rd, wr, lambda e: e.tensor_copy(out, in_))
 
+    def fill(out, x, rd, wr):
+        op("v", rd, wr, lambda e: e.memset(out, x))
+
     def act(out, in_, f, rd, wr, **kw):
         op("s", rd, wr, lambda e: e.activation(out, in_, f, **kw))
 
-    def mm(bank, out, terms, first=True, final=True):
-        for n, (lt, rhs, rd) in enumerate(terms):
+    def mm(bank, terms, first=True, final=True):
+        for n, (out, lt, rhs, rd) in enumerate(terms):
             op("p", rd, [bank],
                lambda e: e.matmul(out, lt, rhs, first and n == 0, final and n == len(terms) - 1))
 
@@ -140,14 +151,15 @@ def rank_program(g, core, T, topo):
             lands(prv, "a%s%d" % (k, (rank - s) % NR), "r%s%d" % (k, (rank - s) % NR))
     if rank == 0:
         for t in range(1, NR):
-            lands((-t) % NR, "ka%d" % t, "kb%d" % t)
+            lands((-t) % NR, "kA%d" % t, "kA%d" % t, "kZ%d" % t)
     else:
         for t in range(1, NT):
-            lands(prv, "ka%d" % t, "kb%d" % t)
+            lands(prv, "kA%d" % t, "kA%d" % t)
+            lands(prv, "kZ%d" % t, "kZ%d" % t)
             lands(prv, "ma%d" % t, "mk%d" % t)
 
     dma("s", "lat", [], ["ats"], T.ats[:], T.at[:])
-    dma("s", "lk0", [], ["k0i"], T.k0i[:], T.key0[:])
+    dma("y", "lk0", [], ["k0i"], T.k0i[:], T.key0[:])
     dma("y", "lch", [], ["chi"], T.chi[:], T.ch[:])
     dma("y", "lrec", [], ["recs"], T.recs[:, 0:R], T.rec[:])
     iota(T.pi[:, 0:1], [[0, 1]], 0, 1, ["pi0"], False)
@@ -156,235 +168,273 @@ def rank_program(g, core, T, topo):
     dma("g", "lsm", [], ["thi"], T.thi[:, 0:1], T.th[:], allow_slow_non_contiguous=True)
     dma("g", "lsm", [], ["wi"], T.wi[:, 0:1], T.w[:], allow_slow_non_contiguous=True)
     wrote["thi"] = wrote["wi"]
-    iota(T.rel[:, 0:192], [[0, 6], [1, 32]], -16, 0, ["rela"], True)
-    iota(T.rel[:, 192:288], [[0, 6], [1, 16]], 0, 0, ["relb"], True)
-    iota(T.eoi[:, 0:12], [[2, 6], [0, 2]], 1, 0, ["eoia"], False)
-    iota(T.eoi[:, 12:18], [[2, 6]], 0, 0, ["eoib"], False)
+    iota(T.rel[:, 0, 0:33], [[1, 33]], 0, 0, ["rela"], True)
+    iota(T.rel[:, 0, 33:50], [[1, 17]], 0, 0, ["relb"], True)
+    iota(T.eoi[:, 0:12], [[2, 6], [0, 2]], 0, 0, ["eoia"], False)
+    iota(T.eoi[:, 12:18], [[2, 6]], 1, 0, ["eoib"], False)
     iota(T.jf[:, 192:V], [[1, V - 192]], 192, 0, ["jfb"], True)
 
     def c(k):
         return T.col[:, k:k + 1]
-    P, GB, U, OD, G15, U1, SC, SI, SB, D0, D1, TH, WT, X0, X1, X2, X3 = range(17)
+    P, GB, U, G15, U1, D1, TH, WT, EB, RV, UR = range(11)
     j = T.jf[:, 0:128]
     ts(T.pi[:, 1:2], T.pi[:, 0:1], 112, None, A.bitwise_and, None, ["pi0"], ["pi1"])
     ts(T.pi[:, 2:3], T.pi[:, 0:1], 15, None, A.bitwise_and, None, ["pi0"], ["pi2"])
-    ts(T.pi[:, 3:4], T.pi[:, 0:1], 1, None, A.bitwise_and, None, ["pi0"], ["pi3"])
-    op("v", [], ["keyf"], lambda e: e.memset(T.keyf[:], 0.0))
-    op("v", [], ["spare"], lambda e: e.memset(T.tab[:, 0:SP], 0.0))
-    cp(T.col[:, 0:4], T.pi[:, 0:4], ["pi0", "pi1", "pi2", "pi3"], ["c0"])
+    fill(T.keyf[:], 0.0, [], ["keyf"])
+    fill(T.tab[:, 0:SP], 0.0, [], ["spare"])
+    fill(T.zero[:], 0.0, [], ["zero"])
+    cp(T.col[:, 0:3], T.pi[:, 0:3], ["pi0", "pi1", "pi2"], ["c0"])
+    cp(T.dm[:], T.jf[:, 0:L], ["jfa"], ["dmA", "dmZ"])
+    ts(c(UR), c(U), -1.0, 191.0, A.mult, A.add, ["c0"], ["ur"])
     ts(c(G15), c(GB), 15.0, None, A.add, None, ["c0"], ["g15"])
     ts(c(U1), c(U), 1.0, None, A.add, None, ["c0"], ["u1"])
-    ts(c(X0), c(U), 15.0, 4095.0, A.is_equal, A.mult, ["c0"], ["x0"])
-    ts(c(X1), c(U), 8.0, -192.0, A.mult, A.add, ["c0"], ["x1"])
-    ts(c(D0), c(U), 16.0, None, A.add, None, ["c0"], ["d0"])
-    ts(c(D1), c(U), 32.0, None, A.add, None, ["c0"], ["d1"])
-    ts(T.bm[:], T.jf[:, 0:144], c(G15), None, A.is_equal, None, ["jfa", "g15"], ["bm"])
-    ts(c(SI), c(X0), 1.0, None, A.add, None, ["x0"], ["si"])
-    ts(c(SC), c(X0), -1.0 / 4096, 1.0, A.mult, A.add, ["x0"], ["sc"])
-    ts(c(X2), c(X1), c(OD), None, A.mult, None, ["x1", "c0"], ["x2"])
-    ts(c(SB), c(SC), float(SP), None, A.mult, None, ["sc"], ["sb"])
-    ts(c(X3), c(X2), c(X1), 399.0, A.add, A.add, ["x2", "x1"], ["x3"])
+    ts(c(D1), c(U), 16.0, None, A.add, None, ["c0"], ["d1"])
+    ts(T.rv[:], T.jf[:, 0:12], -16.0, c(UR), A.mult, A.add, ["jfa", "ur"], ["rv"])
+    ts(c(RV), c(G15), c(U), None, A.subtract, None, ["g15", "c0"], ["crv"])
+    ts(c(EB), c(U), -256.0, float(1 + 2048 * 190 + 128), A.mult, A.add, ["c0"], ["eb"])
     ts(T.i1[:], j, c(P), None, A.is_equal, None, ["jfa", "c0"], ["i1"])
-    ts(T.ao[:, 0:1], c(X3), 287.0, None, A.min, None, ["x3"], ["ao"])
 
+    cp(T.atr[:], T.ats[:, 0:L].indirect(T.rv[:]), ["ats", "rv"], ["atr"])
+    ts(T.prv[:], j, c(RV), None, A.is_equal, None, ["jfa", "crv"], ["prv"])
+    cp(T.k0h[:], T.k0i[:], ["k0i"], ["k0h"])
+    ts(T.bm[:], T.jf[:, 0:144], c(G15), None, A.is_equal, None, ["jfa", "g15"], ["bm"])
+    for k in range(12):
+        mm("b6", [(T.b6[:, k:k + 1], T.prv[:], T.k0h[:, 11 - k:12 - k], ["prv", "k0h"])])
     for i in range(16):
         o = T.ar[:, rank * W + i:(rank + 1) * W:16]
         if i % 2 == 1:
-            act(o, T.ats[:], F.Copy, ["ats"], ["own%d" % i])
+            act(o, T.atr[:], F.Copy, ["atr"], ["own%d" % i])
         else:
-            cp(o, T.ats[:], ["ats"], ["own%d" % i])
+            cp(o, T.atr[:], ["atr"], ["own%d" % i])
     own = ["own%d" % i for i in range(16)]
-
-    ts(T.t1[:], T.rel[:], c(U), -2.0, A.is_equal, A.mult, ["rela", "relb", "c0"], ["t1"])
-    act(T.t3[:], T.t1[:], F.Identity, ["t1"], ["t3"], bias=1.0)
-    for out, src, f, nm in ((T.im1[:], T.i1[:], -1.0, "im1"), (T.i32[:], T.i1[:], 1.0, "i32"),
-                            (T.im2[:], T.i1[:], -2048.0, "im2"), (T.im8[:], T.i1[:], -8192.0, "im8"),
-                            (T.s8f[:], T.i1[:, 0:128:16], 1.0, "s8f"), (T.s8b[:], T.i1[:, 0:128:16], 2048.0, "s8b"),
-                            (T.bo[:], T.bm[:], 128.0, "bo"), (T.b15[:], T.bm[:, 0:128], 128.0 / 4096, "b15"),
-                            (T.jrow[:], T.jf[:, 0:L], 1.0 / 2048, "jrow")):
-        act(out, src, F.Identity, ["i1", "bm", "jfa"], [nm], scale=f)
-    ts(T.t2[:], T.rel[:], c(U1), 4096.0, A.is_equal, A.mult, ["rela", "relb", "u1"], ["t2"])
-    ts(T.i37[:], j, c(P), 37.0, A.is_equal, A.mult, ["jfa", "c0"], ["i37"])
-    ts(T.ones[:], T.j16[:], c(GB), None, A.is_equal, None, ["j16", "c0"], ["ones"])
-    ts(T.qb[:, 0:128], j, c(P), -8192.0, A.is_gt, A.mult, ["jfa", "c0"], ["qb"])
-    ts(T.wn[:, 0:128], j, c(P), 4096.0, A.is_equal, A.mult, ["jfa", "c0"], ["wn"])
-    cp(T.eo[:], T.eoi[:], ["eoia", "eoib"], ["eo"])
-    tt(T.qb[:, 0:128], T.qb[:, 0:128], T.wn[:, 0:128], A.add, ["qb", "wn"], ["qb"])
-    tt(T.cpat[:], T.t3[:], T.t2[:], A.add, ["t3", "t2"], ["cpat"])
-    tt(T.lz[:], T.qb[:, 0:128], T.ones[:], A.mult, ["qb", "ones"], ["lz"])
-    op("v", [], ["cpat"], lambda e: e.memset(T.cpat[:, 0:192:32], 0.0))
-    op("v", [], ["cpat"], lambda e: e.memset(T.cpat[:, 192:288:16], 0.0))
-
-    cp(T.kb[:, 0:12], T.k0i[:], ["k0i"], ["kb0"])
+    cp(T.kb[:, 0:12], T.b6[:, 0:12], ["b6"], ["kA0", "kZ0"])
     if rank != 0:
         t0 = (-rank) % NR
-        send(0, "ka%d" % t0, ["kb0"], T.kb[:, 32 * t0:32 * t0 + 12], T.kb[:, 0:12])
+        send(0, "kA%d" % t0, ["kA0"], T.kb[:, 32 * t0:32 * t0 + 12], T.kb[:, 0:12])
+
+    ts(T.t1[:], T.rel[:], c(U), -1.0, A.is_equal, A.mult, ["rela", "relb", "c0"], ["t1"])
+    ts(T.t2[:], T.rel[:], c(U1), -2.0, A.is_equal, A.mult, ["rela", "relb", "u1"], ["t2"])
+    for out, src, f, nm in ((T.im1[:], T.i1[:], -1.0, "im1"), (T.in2[:], T.i1[:], -2.0, "in2"),
+                            (T.i64[:], T.i1[:], 64.0, "i64"), (T.i32[:], T.i1[:], 1.0, "i32"),
+                            (T.im2[:], T.i1[:], -2048.0, "im2"), (T.im4[:], T.i1[:], -4096.0, "im4"),
+                            (T.im8[:], T.i1[:], -8192.0, "im8"), (T.bo[:], T.bm[:], 128.0, "bo"),
+                            (T.s8f[:], T.i1[:, 0:128:16], 1.0, "s8f"), (T.s8b[:], T.i1[:, 0:128:16], 2048.0, "s8b")):
+        act(out, src, F.Identity, ["i1", "bm"], [nm], scale=f)
+    act(T.t1[:], T.t1[:], F.Identity, ["t1"], ["t1"], bias=1.0)
+    ts(T.i37[:], j, c(P), 37.0, A.is_equal, A.mult, ["jfa", "c0"], ["i37"])
+    ts(T.i16[:], j, c(P), None, A.is_equal, None, ["jfa", "c0"], ["i16"])
+    ts(T.ones[:], T.j16[:], c(GB), None, A.is_equal, None, ["j16", "c0"], ["ones"])
+    ts(T.on2[:], T.j16[:], c(GB), -2.0, A.is_equal, A.mult, ["j16", "c0"], ["on2"])
+    ts(T.qb[:, 0:128], j, c(P), -8192.0, A.is_gt, A.mult, ["jfa", "c0"], ["qbA", "qbZ"])
+    ts(T.wn[:, 0:128], j, c(P), 4096.0, A.is_equal, A.mult, ["jfa", "c0"], ["wn"])
+    cp(T.eo[:], T.eoi[:], ["eoia", "eoib"], ["eo"])
+    for t in range(NT):
+        ts(T.tags[:, L * t:L * t + L], T.dm[:], float(L * t - (960 if t < 5 else 959)), 1.0 / 2048, A.add, A.mult,
+           ["dmA", "dmZ"], ["tag%d" % t])
+        if t == 1:
+            tt(T.qb[:, 0:128], T.qb[:, 0:128], T.wn[:, 0:128], A.add, ["qbA", "wn"], ["qbA", "qbZ"])
+        if t == 3:
+            tt(T.dpat[:], T.t1[:], T.t2[:], A.add, ["t1", "t2"], ["dpat"])
+        if t == 5:
+            tt(T.lz[:], T.qb[:, 0:128], T.ones[:], A.mult, ["qbA", "ones"], ["lz"])
+        if t == 7:
+            ts(T.dpat[:, :, 32:50:17], T.dpat[:, :, 32:50:17], 4096.0, None, A.mult, None, ["dpat"], ["dpat"])
 
     tabw = T.tab[:, SP:SP + V]
-    lo = [HL + sum(CH[:k]) for k in range(len(CH) + 1)]
+    part = {"A": (0, NA), "Z": (NA, L)}
+    bank = {"dA": "b0", "dZ": "b1", "kA": "b6", "kZ": "b7", "cA": "b3", "cZ": "b4", "uA": "b2", "uZ": "b5"}
 
-    def marks(t, fresh, kl, kbn, mo):
-        if fresh:
-            tt(mo, tabw.indirect(kl), T.val[:], A.is_equal, ["tab", kbn, "val"], ["mo%d" % t])
-        else:
-            tt(T.wn[:], tabw.indirect(kl), T.val[:], A.is_equal, ["tab", kbn, "val"], ["wn"])
-            mm("pm", T.pm[:, 0:L], [(T.i1[:], T.mkb[:, t], ["i1", "mk%d" % t]), (T.i1[:], T.wn[:], ["i1", "wn"])])
-            act(mo, T.pm[:, 0:L], F.Sign, ["pm"], ["mo%d" % t])
-
-    for t in range(NT):
+    def step(nm, t):
         home = (rank - t) % NR
         fresh = t == 0 or rank == 0
         last = t == NT - 1
         hand_on = last or rank != NR - 1
         kt = t % NR if rank == 0 else t
-        kl, kbn, mkn = T.kb[:, 32 * kt:32 * kt + 12], "kb%d" % kt, "mk%d" % t
+        kl, kbn, mkn = T.kb[:, 32 * kt:32 * kt + 12], ["kA%d" % kt, "kZ%d" % kt], "mk%d" % t
         arn = own if home == rank else ["ra%d" % home, "rb%d" % home]
-        mo = T.mko[:, L * t:L * t + L]
-        ahead = (rank - t - 1) % NR
-
-        if t == 0:
-            cp(T.cand[:], T.chi[:, 0:V].indirect(kl), ["chi", kbn], ["cand"])
-        else:
-            cp(T.cand[:], tabw.indirect(kl), ["tab", kbn], ["cand"])
-        if kt == t:
-            cp(T.kb[:, 32 * kt + 12:32 * kt + 18], T.kb[:, 32 * kt:32 * kt + 12:2], [kbn], [kbn + "e"])
-        if t == 0:
-            H = V // 2
-            for h in range(2):
-                cp(T.tab[:, SP + V + h * H:SP + V + (h + 1) * H], T.chi[:, h * H:(h + 1) * H], ["chi"], ["ch0%d" % h])
-                act(T.tab[:, SP + h * H:SP + (h + 1) * H], T.tab[:, SP + V + h * H:SP + V + (h + 1) * H], F.Copy,
-                    ["ch0%d" % h], ["tab%d" % h])
-            wrote["tab"], wrote["ch0"] = wrote["tab1"], wrote["ch01"]
-            order("g", ["recs"], [])
-            forward(rank, 0, own)
-            forward(rank, 1, own)
-            dma("y", "lext", ["recs"], ["rece"], T.recs[:, R:R + V], T.rec[:, 0:V])
-
-        recw = T.recs[:, 0:R] if t == 0 else T.recs[:, 0:R + V]
-        recn = ["recs"] if t == 0 else ["recs", "rece"]
-        tag = (L * t - (960 if t < 5 else 959)) / 2048.0
-
-        act(T.xh[:, 0:16 * HL], recw.indirect(T.cand[:, 0:HL]), F.Copy, recn + ["cand"], ["xh"])
-        mm("pv", T.pv[:, 0:16 * HL], [(T.i1[:], T.xh[:, 0:16 * HL], ["i1", "xh"]),
-                                      (T.im1[:], T.ar[:, home * W:home * W + 16 * HL], ["im1"] + arn)])
-        act(T.krow[:], T.jf[:, 0:V].indirect(T.kb[:, 32 * kt:32 * kt + 18]), F.Identity,
-            ["jfa", "jfb", kbn, kbn + "e", "sc", "sb"], ["krow"], bias=c(SB), scale=c(SC))
-        act(T.df[:, 0:16 * HL], T.pv[:, 0:16 * HL], F.Abs, ["pv"], ["dfh"])
-
-        def step(nm):
-            if nm[0] in "vsp" and nm[1:].isdigit():
-                k, k2 = int(nm[1]), int(nm[-1])
-                a, b = lo[k], lo[k2 + 1]
-                if nm[0] == "v":
-                    tt(T.df[:, 16 * a:16 * b], recw.indirect(T.cand[:, a:b]),
-                       T.ar[:, home * W + 16 * a:home * W + 16 * b], A.subtract, recn + ["cand"] + arn, ["df%d" % k])
-                elif nm[0] == "s":
-                    act(T.df[:, 16 * a:16 * b], T.df[:, 16 * a:16 * b], F.Abs, [], ["df%d" % k])
-                else:
-                    a = 0 if k == 0 else a
-                    rd = ["bm"] + ["df%d" % q for q in range(k, k2 + 1)] + (["dfh"] if k == 0 else [])
-                    mm("pd", T.pd[:, a:b], [(T.bm[:, 15 - i:143 - i], T.df[:, 16 * a + i:16 * b:16], rd)
-                                            for i in range(16)])
-            elif nm == "pl":
-                if not fresh:
-                    mm("pm", T.pm[:, 0:12], [(T.bo[:, 15 - u:143 - u] if u < 15 else T.b15[:], T.mkb[:, t, :, u],
-                                              ["bo", "b15", mkn]) for u in range(16)])
-            elif nm == "pre":
-                mm("py", T.py[:, 0:L], [(T.i1[:], T.jrow[:], ["i1", "jrow"])], True, False)
-                if not fresh:
-                    mm("pc", T.pc[:, 320:512], [(T.i1[:], T.mkb[:, t], ["i1", mkn])], True, False)
-                    mm("pc", T.pc[:, 512:608], [(T.i1[:], T.mkb[:, t, 0:12:2, :], ["i1", mkn])], True, False)
-                    mm("pu", T.pu[:, 0:L], [(T.im8[:], T.mkb[:, t], ["im8", mkn])], True, False)
-            elif nm == "keyf":
-                ts(T.keyf[:, 0:12], kl, float(SP), c(SC), A.add, A.mult, [kbn, "sc"], ["keyf"])
-                if t == 0:
-                    cp(c(TH), T.thi[:, 0:1], ["thi"], ["th"])
-                    cp(c(WT), T.wi[:, 0:1], ["wi"], ["wt"])
-                    ts(T.bw[:], T.jf[:, 0:144], c(G15), c(WT), A.is_equal, A.mult, ["jfa", "g15", "wt"], ["bw"])
-            elif nm == "o2":
-                if not fresh:
-                    tt(T.o2f[:], T.pm[:, 0:12], T.keyf[:, 0:12], A.add, ["pm", "keyf"], ["o2f"])
-                    ts(T.o2[:], T.o2f[:], c(SI), -float(SP), A.mult, A.add, ["o2f", "si"], ["o2"])
-            elif nm == "r1":
-                if fresh:
-                    act(T.r1[:], tabw.indirect(kl), F.Identity, ["tab", kbn], ["r1"], bias=MAGIC)
-                else:
-                    act(T.r1[:], T.tab[:, SP:SP + 2 * V].indirect(T.o2[:]), F.Identity, ["tab", "ch0", "o2"], ["r1"],
-                        bias=MAGIC)
-            elif nm == "eq":
-                tt(T.eq[:], T.keyf[:, 0:16].indirect(T.eo[:]), T.krow[:], A.is_equal, ["keyf", "eo", "krow"], ["eq"])
-            elif nm == "cc":
-                act(T.c1[:], T.r1[:], F.Identity, ["r1"], ["c1"], bias=-MAGIC)
-            elif nm == "sgw":
-                act(T.sgw[:], T.c1[:], F.Sign, ["c1"], ["sgw"], bias=-4095.5)
-            elif nm == "yc":
-                mm("py", T.py[:, 0:L], [(T.i32[:], T.c1[:], ["i32", "c1"])], False, False)
-            elif nm == "py":
-                mm("py", T.py[:, 0:L], [(T.im2[:], T.sgw[:], ["im2", "sgw"])], False, True)
-            elif nm == "yv":
-                act(T.yv[:], T.py[:, 0:L], F.Identity, ["py"], ["yv"], bias=-2048.0 + tag)
-            elif nm == "fl":
-                ts(T.fl[:], T.pd[:, 0:L], c(TH), None, A.is_gt, None, ["pd", "th"], ["fl"])
-            elif nm == "dm":
-                ts(T.dm[:], T.pd[:, 0:L], -2048.0, None, A.add, None, ["pd"], ["dm"])
-            elif nm == "qb":
-                act(T.qb[:], T.pd[:, 0:L], F.Identity, ["pd"], ["qb"], scale=37.0 / 2048, bias=155.0 - 1022.5 / 2048)
-            elif nm == "pc":
-                mm("pc", T.pc[:, 320:512], [(T.ones[:], T.fl[:], ["ones", "fl"])], fresh, True)
-                mm("pc", T.pc[:, 512:608], [(T.ones[:], T.fl[:, 0:12:2, :], ["ones", "fl"])], fresh, True)
-            elif nm == "pu":
-                mm("pu", T.pu[:, 0:L], [(T.lz[:], T.fl[:], ["lz", "fl"]), (T.i37[:], T.dm[:], ["i37", "dm"]),
-                                        (T.im2[:], T.qb[:], ["im2", "qb"])], fresh, True)
-            elif nm == "ef":
-                act(T.ef[:], T.pu[:, 0:L], F.Relu, ["pu"], ["ef"], bias=float(1 + 2048 * 192 - 4096))
-            elif nm == "pp":
-                tt(T.pp[:], T.pc[:, 320:608], T.eq[:], A.min, ["pc", "eq"], ["pp"])
-            elif nm == "rr":
-                op("v", ["cpat", "pp"], ["rr"],
-                   lambda e: e.tensor_tensor_scan(T.rr[:], T.cpat[:], T.pp[:], 0.0, A.mult, A.add))
-            elif nm == "mm":
-                tt(T.mm[:], T.rr[:, 0:288].indirect(T.ao[:, 0:1]), T.keyf[:], A.min, ["rr", "ao", "keyf"], ["mm"])
-            elif nm == "off":
-                ts(T.off[:, 0:12:2], T.mm[:, 0:12:2], c(SI), c(D0), A.mult, A.max, ["mm", "si", "d0"], ["off0"])
-                ts(T.off[:, 1:12:2], T.mm[:, 1:12:2], c(SI), c(D1), A.mult, A.max, ["mm", "si", "d1"], ["off1"])
-            elif nm == "fwd":
-                if t < NR - 2:
-                    forward(ahead, 0, ["ra%d" % ahead])
-            elif not hand_on:
-                pass
-            elif nm == "pk":
-                mm("pk", T.pk[:, 0:12], [(T.bw[:, 15 - u:143 - u], T.dm[:, u:L:16], ["bw", "dm"]) for u in range(16)])
-            elif nm == "ki":
-                cp(T.ki[:], T.pk[:, 0:12], ["pk"], ["ki"])
-            elif nm == "kj":
-                ts(T.kj[:], T.ki[:], V - 1, None, A.bitwise_and, None, ["ki"], ["kj"])
-            elif nm == "ko":
-                cp(T.ko[:, 16 * t:16 * t + 12], T.kj[:], ["kj"], ["ko%d" % t])
-                if not last:
-                    send(nxt, "ka%d" % (t + 1), ["ko%d" % t], T.kb[:, 32 * (t + 1):32 * (t + 1) + 12],
-                         T.ko[:, 16 * t:16 * t + 12])
-            elif nm == "val":
-                mm("pv", T.pv[:, 0:L], [(T.i32[:], T.yv[:], ["i32", "yv"]), (T.i32[:], T.ef[:], ["i32", "ef"])])
-                act(T.val[:], T.pv[:, 0:L], F.Copy, ["pv"], ["val"])
-        for nm in ORDER.split():
-            step(nm)
-
-        for p in range(5, -1, -1):
+        mo, mk = T.mko[:, L * t:L * t + L], T.mkb[:, t]
+        recw = T.recs[:, 0:min(R + t * V, 2 * R)]
+        recn = ["recs", "rece", "recf"][:t + 1]
+        z = nm[-1]
+        a, b = part.get(z, (0, L))
+        sl, ca, cb, pa, pb = slice(a, b), a // 16, b // 16, a // 32, b // 32
+        if nm[:4] == "cand":
+            src = T.chi[:, 0:V] if t == 0 else tabw
+            cp(T.cand[:, sl], src.indirect(T.kb[:, 32 * kt + ca:32 * kt + cb]),
+               ["chi" if t == 0 else "tab", "k%s%d" % (z, kt)], [nm])
+            if t == 0 and z == "A":
+                H = V // 2
+                for h in range(2):
+                    ts(T.tab[:, SP + V + h * H:SP + V + (h + 1) * H], T.chi[:, h * H:(h + 1) * H], float(R), None,
+                       A.add, None, ["chi"], ["ch0%d" % h])
+                    act(T.tab[:, SP + h * H:SP + (h + 1) * H], T.tab[:, SP + V + h * H:SP + V + (h + 1) * H],
+                        F.Identity, ["ch0%d" % h], ["tab%d" % h], bias=-float(R))
+                wrote["tab"], wrote["ch0"] = wrote["tab1"], wrote["ch01"]
+                order("g", ["recs"], [])
+                forward(rank, 0, own)
+                forward(rank, 1, own)
+                dma("y", "lext", ["recs"], ["rece"], T.recs[:, R:R + V], T.rec[:, 0:V])
+            if t == 1 and z == "A":
+                dma("y", "lex2", ["candA"], ["recf"], T.recs[:, R + V:2 * R], T.rec[:, V:R])
+        elif nm == "xh":
+            act(T.xh[:, 0:16 * CUT[1]], recw.indirect(T.cand[:, 0:CUT[1]]), F.Copy, recn + ["candA"], ["xh"])
+        elif nm == "pv":
+            n = 16 * CUT[1]
+            mm("b2", [(T.b2[:, 0:n], T.im1[:], T.ar[:, home * W:home * W + n], ["im1"] + arn),
+                      (T.b2[:, 0:n], T.i1[:], T.xh[:, 0:n], ["i1", "xh"])])
+        elif nm == "s0":
+            act(T.df[:, 0:16 * CUT[1]], T.b2[:, 0:16 * CUT[1]], F.Abs, ["b2"], ["df0"])
+        elif nm[0] in "vs" and nm[1:].isdigit():
+            k = int(nm[1:])
+            a, b = CUT[k], CUT[k + 1]
+            if nm[0] == "v":
+                tt(T.df[:, 16 * a:16 * b], recw.indirect(T.cand[:, a:b]), T.ar[:, home * W + 16 * a:home * W + 16 * b],
+                   A.subtract, recn + ["candA" if a < NA else "candZ"] + arn, ["df%d" % k])
+            else:
+                act(T.df[:, 16 * a:16 * b], T.df[:, 16 * a:16 * b], F.Abs, ["df%d" % k], ["df%d" % k])
+        elif nm[0] == "d" and z.isdigit():
+            a, b = DCUT[int(z)], DCUT[int(z) + 1]
+            rd = ["bm"] + ["df%d" % k for k in range(len(CUT) - 1) if CUT[k] < b and CUT[k + 1] > a]
+            d = bank["dA" if a < NA else "dZ"]
+            mm(d, [(T[d][:, a:b], T.bm[:, 15 - i:143 - i], T.df[:, 16 * a + i:16 * b:16], rd) for i in range(16)])
+        elif nm == "krow":
+            act(T.krow[:], T.jf[:, 0:V].indirect(T.kb[:, 32 * kt:32 * kt + 18]), F.Identity,
+                ["jfa", "jfb", "kE%d" % kt] + kbn, ["krow"], bias=float(SP))
+        elif nm == "kex":
+            if kt == t:
+                cp(T.kb[:, 32 * kt + 12:32 * kt + 18], T.kb[:, 32 * kt + 1:32 * kt + 12:2], kbn, ["kE%d" % kt])
+        elif nm == "keyf":
+            ts(T.keyf[:, 0:12], kl, float(SP), None, A.add, None, kbn, ["keyf"])
+            if t == 0:
+                cp(c(TH), T.thi[:, 0:1], ["thi"], ["th"])
+                cp(c(WT), T.wi[:, 0:1], ["wi"], ["wt"])
+                ts(T.bw[:], T.jf[:, 0:144], c(G15), c(WT), A.is_equal, A.mult, ["jfa", "g15", "wt"], ["bw"])
+        elif nm == "eq":
+            tt(T.ne[:], T.keyf[:, 0:16].indirect(T.eo[:]), T.krow[:], A.not_equal, ["keyf", "eo", "krow"], ["ne"])
+        elif nm == "pl":
+            if not fresh:
+                mm("b6", [(T.b6[:, 32:44], T.i32[:], T.keyf[:, 0:12], ["i32", "keyf"])]
+                   + [(T.b6[:, 32:44], T.bo[:, 15 - u:143 - u], T.mkb[:, t, :, u:32:16], ["bo", mkn])
+                      for u in range(16)])
+        elif nm == "o2":
+            if not fresh:
+                ts(T.o2[:], T.b6[:, 32:44], -float(SP), None, A.add, None, ["b6"], ["o2"])
+        elif nm == "r1":
+            if fresh:
+                act(T.r1[:], tabw.indirect(kl), F.Identity, ["tab"] + kbn, ["r1"], bias=MAGIC)
+            else:
+                act(T.r1[:], T.tab[:, SP:SP + 2 * V].indirect(T.o2[:]), F.Identity, ["tab", "ch0", "o2"], ["r1"],
+                    bias=MAGIC)
+        elif nm == "c1":
+            act(T.c1[:], T.r1[:], F.Identity, ["r1"], ["c1"], bias=-MAGIC)
+        elif nm == "wf":
+            ts(T.wf[:], T.cand[:], 4095.5, None, A.is_gt, None, ["candA", "candZ"], ["wf"])
+        elif nm == "py":
+            mm("b7", [(T.b7[:, 256:256 + L], T.i16[:], T.tags[:, L * t:L * t + L], ["i16", "tag%d" % t]),
+                      (T.b7[:, 256:256 + L], T.im4[:], T.wf[:], ["im4", "wf"])])
+        elif nm == "yv":
+            tt(T.yv[:], T.b7[:, 256:256 + L], T.c1[:], A.add, ["b7", "c1"], ["yv"])
+        elif nm[:2] == "dm":
+            ts(T.dm[:, sl], T[bank["d" + z]][:, sl], -2048.0, None, A.add, None, [bank["d" + z]], [nm])
+        elif nm[:2] == "fl":
+            ts(T.fl[:, pa:pb], T[bank["d" + z]][:, sl], c(TH), 1.0 / 32, A.is_gt, A.subtract,
+               [bank["d" + z], "th"], [nm])
+        elif nm[:2] == "qb":
+            act(T.qb[:, sl], T[bank["d" + z]][:, sl], F.Identity, [bank["d" + z]], [nm], scale=37.0 / 2048,
+                bias=155.0 - 1022.5 / 2048)
+        elif nm[:2] in ("pc", "pu") or nm[:3] == "pre":
+            pc, pu, n = T[bank["c" + z]], T[bank["u" + z]][:, sl], pb - pa
+            early = {"c": [(pc[:, 0:n, 0:50], T.i64[:], T.zero[:, 0:50 * n], ["i64", "zero"]),
+                           (pc[:, 0:n, 0:32], T.i64[:], T.ne[:, sl], ["i64", "ne"]),
+                           (pc[:, 0:n, 33:49], T.i64[:], T.ne[:, L + 16 * pa:L + 16 * pb], ["i64", "ne"]),
+                           (pc[:, 0:n, 32:50:17], T.i32[:], T.keyf[:, ca:cb], ["i32", "keyf"])], "u": []}
+            if not fresh:
+                early["c"] += [(pc[:, 0:n, 0:32], T.in2[:], T.mkb[:, t, pa:pb], ["in2", mkn]),
+                               (pc[:, 0:n, 33:49], T.in2[:], T.mkb[:, t, pa:pb, 16:32], ["in2", mkn])]
+                early["u"] += [(pu, T.im8[:], T.mkb[:, t, pa:pb], ["im8", mkn])]
+            late = {"c": [(pc[:, 0:n, 0:32], T.on2[:], T.fl[:, pa:pb], ["on2", "fl" + z]),
+                          (pc[:, 0:n, 33:49], T.on2[:], T.fl[:, pa:pb, 16:32], ["on2", "fl" + z])],
+                    "u": [(pu, T.lz[:], T.fl[:, pa:pb], ["lz", "fl" + z]), (pu, T.i37[:], T.dm[:, sl], ["i37", "dm" + z]),
+                          (pu, T.im2[:], T.qb[:, sl], ["im2", "qb" + z])]}
+            if nm[:3] == "pre":
+                for k in "cu":
+                    mm(bank[k + z], early[k], True, False)
+            elif "pre" + z in ORDER.split():
+                mm(bank[nm[1:]], late[nm[1]], not early[nm[1]], True)
+            else:
+                mm(bank[nm[1:]], early[nm[1]] + late[nm[1]])
+        elif nm[:2] == "ef":
+            act(T.ef[:, sl], T[bank["u" + z]][:, sl], F.Relu, [bank["u" + z], "eb"], [nm], bias=c(EB))
+        elif nm[:2] == "rr":
+            for p in range(pa, pb):
+                op("v", ["dpat", bank["c" + z]], ["rr%d" % p],
+                   lambda e: e.tensor_tensor_scan(T.rr[:, p], T.dpat[:, 0], T[bank["c" + z]][:, p - pa, 0:50], 0.0,
+                                                  A.mult, A.min))
+        elif nm[:3] == "off":
+            rd = ["rr%d" % p for p in range(pa, pb)]
+            ts(T.off[:, ca:cb:2], T.rr[:, pa:pb, 32], c(U), None, A.max, None, rd + ["c0"], [nm + "0"])
+            ts(T.off[:, ca + 1:cb:2], T.rr[:, pa:pb, 49], c(D1), None, A.max, None, rd + ["d1"], [nm + "1"])
+        elif nm[:2] == "sc":
+            p = int(z)
+            y = "A" if 32 * p < NA else "Z"
             tt(T.tab[:, 0:SP + V].indirect(T.off[:, 2 * p:2 * p + 2]), T.yv[:, 32 * p:32 * p + 32],
-               T.ef[:, 32 * p:32 * p + 32], A.add, ["off0", "off1", "yv", "ef"], ["tab", "spare"])
-        if hand_on and not last:
-            marks(t, fresh, kl, kbn, mo)
-            send(nxt, "ma%d" % (t + 1), ["mo%d" % t], T.mkb[:, t + 1], mo)
-        if t < NR - 2:
-            forward(ahead, 1, ["rb%d" % ahead])
+               T.ef[:, 32 * p:32 * p + 32], A.add, ["off%s0" % y, "off%s1" % y, "yv", "ef" + y], ["tab", "spare"])
+        elif nm == "fwd":
+            ahead = (rank - t) % NR
+            if 0 < t < NR - 1:
+                forward(ahead, 0, ["ra%d" % ahead])
+                forward(ahead, 1, ["rb%d" % ahead])
+        elif not hand_on:
+            pass
+        elif nm[:2] == "pk":
+            mm(bank[nm[1:]], [(T[bank[nm[1:]]][:, ca:cb], T.bw[:, 15 - u:143 - u], T.dm[:, a + u:b:16], ["bw", "dm" + z])
+                              for u in range(16)])
+        elif nm[:2] == "ki":
+            cp(T.ki[:, ca:cb], T[bank["k" + z]][:, ca:cb], [bank["k" + z]], [nm])
+        elif nm[:2] == "kj":
+            ts(T.kj[:, ca:cb], T.ki[:, ca:cb], V - 1, None, A.bitwise_and, None, ["ki" + z], [nm])
+        elif nm[:2] == "ko":
+            o = T.ko[:, 16 * t + ca:16 * t + cb]
+            cp(o, T.kj[:, ca:cb], ["kj" + z], ["o%s%d" % (z, t)])
+            if not last:
+                send(nxt, "k%s%d" % (z, t + 1), ["o%s%d" % (z, t)], T.kb[:, 32 * (t + 1) + ca:32 * (t + 1) + cb], o)
+        elif nm == "wn":
+            tt(T.wn[:], tabw.indirect(kl), T.yv[:], A.is_equal, ["tab", "yv"] + kbn, ["wn"])
+        elif nm == "pm":
+            mm("b5", ([] if fresh else [(T.b5[:, 256:256 + L], T.i1[:], mk, ["i1", mkn])])
+               + [(T.b5[:, 256:256 + L], T.ones[:], T.wn[:], ["ones", "wn"])])
+        elif nm == "mo":
+            act(mo, T.b5[:, 256:256 + L], F.Sign, ["b5"], ["mo%d" % t])
+            if not last:
+                send(nxt, "ma%d" % (t + 1), ["mo%d" % t], T.mkb[:, t + 1], mo)
+        else:
+            raise ValueError(nm)
+
+    for t in range(NT):
+        for nm in ORDER.split():
+            if nm[0] != "<":
+                step(nm, t)
+            elif t > 0:
+                step(nm[1:], t - 1)
+            if nm == "<mo":
+                step("fwd", t)
 
     t = NT - 1
-    banks = ["pu", "py", "pc", "pd", "pv"]
+    banks = ["b1", "b2", "b6", "b7", "b1"]
     cut = [0, 256, 768, 1280, 1792, 2048]
-    for k in range(5):
+    act(T.r1[:], T.jf[:, 0:V].indirect(T.ko[:, 16 * t:16 * t + 12]), F.Identity,
+        ["jfa", "jfb", "oA%d" % t, "oZ%d" % t], ["r1"])
+    step("wn", t)
+    act(T.c1[:], T.r1[:, 0:L].indirect(T.rv[:]), F.Identity, ["r1", "rv"], ["c1"])
+    mm("b0", [(T.b0[0:8, 0:L], T.s8f[:], T.c1[:], ["s8f", "c1"])], True, False)
+    step("pm", t)
+
+    def sign(k):
         a, b = cut[k], cut[k + 1]
         act(T.so[:, a:b], T.tab[:, SP + a:SP + b], F.Sign, ["tab"], ["so%d" % k], bias=-4095.5)
-        mm(banks[k], T[banks[k]][:, 0:b - a], [(T.im2[:], T.so[:, a:b], ["im2", "so%d" % k])])
+        mm(banks[k], [(T[banks[k]][:, 0:b - a], T.im2[:], T.so[:, a:b], ["im2", "so%d" % k])])
+    for k in range(4):
+        sign(k)
     for k in range(6):
         if k < 5:
             a, b = cut[k], cut[k + 1]
@@ -394,12 +444,12 @@ def rank_program(g, core, T, topo):
             tt(T.oc[:, a:b], T[banks[k - 1]][:, 0:b - a], T.ro[:, a:b], A.add, [banks[k - 1], "ro%d" % (k - 1)],
                ["oc%d" % k])
             dma("y", "stored", ["oc%d" % k], [], T.yc[:, a:b], T.oc[:, a:b])
-        if k == 2:
-            marks(t, fresh, kl, kbn, mo)
-    act(T.krow[:, 0:L], T.jf[:, 0:V].indirect(T.ko[:, 16 * t:16 * t + 12]), F.Identity,
-        ["jfa", "jfb", "ko%d" % t], ["krow"])
-    mm("pk", T.pk[0:8, 0:L], [(T.s8f[:], T.krow[:, 0:L], ["s8f", "krow"]), (T.s8b[:], mo, ["s8b", "mo%d" % t])])
-    act(T.yks[0:8, :], T.pk[0:8, 0:L], F.Copy, ["pk"], ["yks"])
-    dma("s", "stored", ["yks"], [], T.yk[:], T.yks[0:8, :])
+        if k == 1:
+            sign(4)
+            step("mo", t)
+            act(T.qb[:], T.mko[:, L * t:L * t + L].indirect(T.rv[:]), F.Copy, ["mo%d" % t, "rv"], ["qbA", "qbZ"])
+            mm("b0", [(T.b0[0:8, 0:L], T.s8b[:], T.qb[:], ["s8b", "qbA"])], False, True)
+            act(T.yks[0:8, :], T.b0[0:8, 0:L], F.Copy, ["b0"], ["yks"])
+            dma("s", "stored", ["yks"], [], T.yk[:], T.yks[0:8, :])
     for sem, n in count.items():
         g.wait_ge(T.sem[sem], n)

@@ -1,39 +1,52 @@
 from concourse.mybir import AluOpType, ActivationFunctionType
 
 NR, NT, L, V, R = 8, 10, 192, 2048, 4096
-SP = 32
-CUT = [0, 32, 64, 96, 128, 160, 180, 192]
-DCUT = [0, 64, 128, 192]
-NA = 128
+NC = 4
+CL = 16 * NC
+SP = CL
+SEG = [(k * (CL + 2) - 8 * k * (k - 1), CL - 16 * k) for k in range(NC)]
+SL = SEG[-1][0] + 18
+CUT = [0, 30, 64, 96, 128, 160, 180, 192]
+BY_S = [0]
+PART = {"X": (0, 64), "Y": (64, 128), "A": (0, 128), "Z": (128, 192)}
+KEYS = "AZ"
+LIST = False
+EARLY = ("candA candZ keyh keyf init krow more x0 wf v1 thw w0 py v2 s1 s0 bw dX v3 s2 v4 s3 dY v5 r1 s4 v6 ne0 ne1 "
+         "preA dmA flA prA pcA rest s5 s6 dZ qbA c1 ksA rrA puA ne2 preZ krA flZ dmZ yv kfA offA efA pcZ koA sc0 rrZ "
+         "prZ ksZ qbZ sc1 krZ puZ efZ offZ kfZ sc2 koZ tag")
 MAGIC = 12582912.0
-ORDER = ("candA <wn <pm xh v1 <mo pv v2 v3 s1 candZ kex keyf wf s0 v4 v6 s2 d0 s3 py krow eq s4 s6 d1 flA dmA pl o2 "
-         "v5 pcA qbA pkA puA rrA r1 kiA offA s5 d2 c1 kjA preZ yv efA koA sc0 flZ pcZ dmZ qbZ puZ efZ sc1 pkZ rrZ "
-         "sc2 offZ sc3 kiZ sc4 kjZ sc5 koZ")
+ORDER = ("candA <wn x0 <pm w0 v2 <mo v3 fwa candZ s2 keyf s3 keyh v1 s0 krow s1 wf dY pl v4 s4 ne1 py dX ne0 o1 v5 v6 "
+         "dmA fwb r1 flA ne2 preA prA s5 ksA pcA rrA s6 qbA krA dZ puA c1 yv preZ efA kfA dmZ flZ offA pcZ koA sc0 "
+         "rrZ prZ qbZ ksZ sc1 krZ offZ puZ efZ kfZ sc2 koZ tag")
 
 BF, F32, F16, I32, U16 = "bfloat16", "float32", "float16", "int32", "uint16"
 SCRATCH = {name: ("sbuf", [128] + shape, dtype) for name, shape, dtype in [
     ("chi", [V], I32), ("recs", [2 * R], BF), ("tab", [SP + 2 * V], F32),
-    ("ats", [L], BF), ("atr", [L], BF), ("ar", [NR * 16 * L], BF), ("df", [16 * L], BF), ("xh", [512], BF),
+    ("ats", [L], BF), ("atr", [L], BF), ("ar", [NR * 16 * L], BF), ("df", [16 * L], BF), ("xh", [1024], BF),
     ("k0i", [12], I32), ("k0h", [12], F16), ("thi", [4], I32), ("wi", [4], I32),
-    ("kb", [NT * 32], U16), ("ko", [NT * 16], U16), ("mkb", [NT, 6, 32], BF), ("mko", [NT * L], BF),
-    ("jf", [V], F32), ("j16", [128], F32), ("rel", [1, 50], BF), ("t1", [50], BF), ("t2", [50], BF),
-    ("pi", [8], I32), ("col", [24], F32), ("eoi", [18], I32), ("eo", [18], U16), ("rvf", [12], F32), ("rv", [12], U16),
+    ("kb", [NT * 32], U16), ("ko", [NT * 16], U16), ("mkb", [NT, L // CL, CL], BF), ("mko", [NT * L], BF),
+    ("jf", [V], F32), ("j16", [128], F32), ("rel", [SL], BF), ("t1", [SL], BF), ("t2", [SL], BF),
+    ("pi", [8], I32), ("col", [24], F32), ("ends", [2], U16), ("rv", [12], U16),
     ("bm", [144], BF), ("bw", [144], F16), ("bo", [144], BF), ("i1", [128], BF), ("im1", [128], BF),
     ("in2", [128], BF), ("i64", [128], BF), ("i32", [128], F32), ("i16", [128], F16), ("i37", [128], F16),
-    ("im2", [128], BF), ("im4", [128], BF), ("im8", [128], BF), ("ones", [128], BF), ("on2", [128], BF),
+    ("im2", [128], BF), ("im4", [128], BF), ("i4", [128], BF), ("imm", [128], BF), ("one", [512], BF),
+    ("im8", [128], BF), ("ones", [128], BF), ("on2", [128], BF),
     ("lz", [128], BF), ("prv", [128], F16), ("s8f", [8], F32), ("s8b", [8], BF),
-    ("tags", [NT * L], F16), ("dpat", [1, 50], BF),
-    ("cand", [L], U16), ("keyf", [16], F32), ("krow", [288], F32), ("ne", [288], BF), ("zero", [300], BF),
-    ("rr", [6, 50], F32),
-    ("off", [12], U16), ("o2", [12], U16), ("r1", [L], F32), ("c1", [L], F32), ("wf", [L], BF), ("yv", [L], F32),
-    ("ef", [L], F32), ("dm", [L], F16), ("fl", [6, 32], BF), ("qb", [L], BF), ("wn", [L], BF),
-    ("ki", [12], I32), ("kj", [12], I32),
+    ("tags", [NT * L], F16), ("dpat", [SL], BF),
+    ("cand", [L], U16), ("keyf", [12], F32), ("keyh", [L // CL, NC], F16), ("krow", [L], F32),
+    ("ne", [L // CL, SL], BF), ("rr", [L // CL * SL], F32), ("off", [32], U16),
+    ("o2", [NT * 16], U16), ("o2o", [NT * 16], U16), ("val", [L], F32), ("r1", [L], F32), ("c1", [L], F32),
+    ("wf", [L], BF), ("yv", [L], F32),
+    ("ef", [L], F32), ("dm", [L], F16), ("fl", [L // CL, CL], BF), ("qb", [L], BF), ("wn", [L], BF),
+    ("kr", [12], F32), ("kf", [12], F32), ("half", [L], F16), ("jh", [L], F16),
+    ("kx", [L], F32), ("kpat", [L], BF), ("kmask", [L], BF), ("r16", [L], BF), ("bwr", [128], F16),
     ("ro", [V], F32), ("so", [V], BF), ("oc", [V], F32), ("yks", [L], F32)]}
 PSUM = ("b0", "b1", "b2", "b3", "b4", "b5", "b6", "b7")
 for _b in PSUM:
-    SCRATCH[_b] = ("psum", [128, 8, 64] if _b in ("b3", "b4") else [128, 512], F32)
+    SCRATCH[_b] = ("psum", [128, 32 // NC ** 2, 16 * NC ** 2] if _b in ("b3", "b4") else [128, 512], F32)
 SEMAPHORES = (["qv", "qs", "qp", "qg", "sent", "lsm", "lch", "lrec", "lext", "lex2", "lk0", "lat", "stored"]
-              + ["k%s%d" % (z, t) for t in range(NT) for z in "AZ"] + ["ma%d" % t for t in range(NT)]
+              + ["k%s%d" % (z, t) for t in range(NT) for z in PART]
+              + ["%s%d" % (z, t) for t in range(NT) for z in ("ma", "oa")]
               + ["aa%d" % h for h in range(NR)] + ["ab%d" % h for h in range(NR)])
 
 A = AluOpType
@@ -151,12 +164,14 @@ def rank_program(g, core, T, topo):
             lands(prv, "a%s%d" % (k, (rank - s) % NR), "r%s%d" % (k, (rank - s) % NR))
     if rank == 0:
         for t in range(1, NR):
-            lands((-t) % NR, "kA%d" % t, "kA%d" % t, "kZ%d" % t)
+            lands((-t) % NR, "kZ%d" % t, *["k%s%d" % (z, t) for z in KEYS])
     else:
         for t in range(1, NT):
-            lands(prv, "kA%d" % t, "kA%d" % t)
-            lands(prv, "kZ%d" % t, "kZ%d" % t)
+            for z in KEYS:
+                lands(prv, "k%s%d" % (z, t), "k%s%d" % (z, t))
             lands(prv, "ma%d" % t, "mk%d" % t)
+            if LIST:
+                lands(prv, "oa%d" % t, "ob%d" % t)
 
     dma("s", "lat", [], ["ats"], T.ats[:], T.at[:])
     dma("y", "lk0", [], ["k0i"], T.k0i[:], T.key0[:])
@@ -168,27 +183,31 @@ def rank_program(g, core, T, topo):
     dma("g", "lsm", [], ["thi"], T.thi[:, 0:1], T.th[:], allow_slow_non_contiguous=True)
     dma("g", "lsm", [], ["wi"], T.wi[:, 0:1], T.w[:], allow_slow_non_contiguous=True)
     wrote["thi"] = wrote["wi"]
-    iota(T.rel[:, 0, 0:33], [[1, 33]], 0, 0, ["rela"], True)
-    iota(T.rel[:, 0, 33:50], [[1, 17]], 0, 0, ["relb"], True)
-    iota(T.eoi[:, 0:12], [[2, 6], [0, 2]], 0, 0, ["eoia"], False)
-    iota(T.eoi[:, 12:18], [[2, 6]], 1, 0, ["eoib"], False)
+    for k, (s, n) in enumerate(SEG):
+        iota(T.rel[:, s:s + n + 2], [[1, n + 2]], 0, 0, ["rel%d" % k], True)
+    iota(T.r16[:], [[0, 12], [1, 16]], 0, 0, ["r16"], True)
     iota(T.jf[:, 192:V], [[1, V - 192]], 192, 0, ["jfb"], True)
 
     def c(k):
         return T.col[:, k:k + 1]
-    P, GB, U, G15, U1, D1, TH, WT, EB, RV, UR = range(11)
+    P, GB, U, KK, KQ, G15, U1, TH, WT, EB, RV, UR, X0, X1, X2 = range(15)
     j = T.jf[:, 0:128]
     ts(T.pi[:, 1:2], T.pi[:, 0:1], 112, None, A.bitwise_and, None, ["pi0"], ["pi1"])
     ts(T.pi[:, 2:3], T.pi[:, 0:1], 15, None, A.bitwise_and, None, ["pi0"], ["pi2"])
-    fill(T.keyf[:], 0.0, [], ["keyf"])
+    ts(T.pi[:, 3:4], T.pi[:, 0:1], NC - 1, None, A.bitwise_and, None, ["pi0"], ["pi3"])
+    ts(T.pi[:, 4:5], T.pi[:, 0:1], 16 - NC, None, A.bitwise_and, None, ["pi0"], ["pi4"])
     fill(T.tab[:, 0:SP], 0.0, [], ["spare"])
-    fill(T.zero[:], 0.0, [], ["zero"])
-    cp(T.col[:, 0:3], T.pi[:, 0:3], ["pi0", "pi1", "pi2"], ["c0"])
-    cp(T.dm[:], T.jf[:, 0:L], ["jfa"], ["dmA", "dmZ"])
+    cp(T.col[:, 0:5], T.pi[:, 0:5], ["pi0", "pi1", "pi2", "pi3", "pi4"], ["c0"])
+    cp(T.jh[:], T.jf[:, 0:L], ["jfa"], ["jh"])
+    for p in range(L // CL):
+        act(T.ne[:, p], T.jf[:, 0:SL], F.Identity, ["jfa"], ["ne"], scale=0.0, bias=16.0)
+        act(T.rr[:, SL * p:SL * p + SL], T.jf[:, 0:SL], F.Identity, ["jfa"], ["rr%d" % p], scale=0.0)
     ts(c(UR), c(U), -1.0, 191.0, A.mult, A.add, ["c0"], ["ur"])
     ts(c(G15), c(GB), 15.0, None, A.add, None, ["c0"], ["g15"])
     ts(c(U1), c(U), 1.0, None, A.add, None, ["c0"], ["u1"])
-    ts(c(D1), c(U), 16.0, None, A.add, None, ["c0"], ["d1"])
+    ts(c(X0), c(KK), 1.0, None, A.add, None, ["c0"], ["x0"])
+    ts(c(X1), c(KK), -8.0, float(CL + 2), A.mult, A.add, ["c0"], ["x1"])
+    ts(c(X2), c(KQ), SL / NC, -1.0, A.mult, A.add, ["c0"], ["x2"])
     ts(T.rv[:], T.jf[:, 0:12], -16.0, c(UR), A.mult, A.add, ["jfa", "ur"], ["rv"])
     ts(c(RV), c(G15), c(U), None, A.subtract, None, ["g15", "c0"], ["crv"])
     ts(c(EB), c(U), -256.0, float(1 + 2048 * 190 + 128), A.mult, A.add, ["c0"], ["eb"])
@@ -207,42 +226,62 @@ def rank_program(g, core, T, topo):
         else:
             cp(o, T.atr[:], ["atr"], ["own%d" % i])
     own = ["own%d" % i for i in range(16)]
-    cp(T.kb[:, 0:12], T.b6[:, 0:12], ["b6"], ["kA0", "kZ0"])
+    cp(T.kb[:, 0:12], T.b6[:, 0:12], ["b6"], ["k%s0" % z for z in KEYS])
     if rank != 0:
         t0 = (-rank) % NR
-        send(0, "kA%d" % t0, ["kA0"], T.kb[:, 32 * t0:32 * t0 + 12], T.kb[:, 0:12])
+        send(0, "kZ%d" % t0, ["kZ0"], T.kb[:, 32 * t0:32 * t0 + 12], T.kb[:, 0:12])
 
-    ts(T.t1[:], T.rel[:], c(U), -1.0, A.is_equal, A.mult, ["rela", "relb", "c0"], ["t1"])
-    ts(T.t2[:], T.rel[:], c(U1), -2.0, A.is_equal, A.mult, ["rela", "relb", "u1"], ["t2"])
+    ts(c(X0), c(X0), c(X1), c(X2), A.mult, A.add, ["x0", "x1", "x2"], ["x0"])
+    for k, (s, n) in enumerate(SEG):
+        ts(T.ne[:, :, s + n + 1], T.jf[:, 0:L // CL], 0.0, c(U), A.mult, A.add, ["jfa", "c0", "ne"], ["nd%d" % k])
+    ts(T.ends[:, 0:1], c(X0), float(L // CL * SL - 1), None, A.min, None, ["x0"], ["ends"])
+    rels = ["rel%d" % k for k in range(NC)]
+    ts(T.t1[:], T.rel[:], c(U), -1.0, A.is_equal, A.mult, rels + ["c0"], ["t1"])
+    ts(T.t2[:], T.rel[:], c(U1), -2.0, A.is_equal, A.mult, rels + ["u1"], ["t2"])
+    for k, (s, n) in enumerate(SEG):
+        ts(T.ne[:, :, s + n + 1], T.ne[:, :, s + n + 1], 16.0 * k, -1.0 / 64, A.add, A.mult, ["nd%d" % k], ["nd%d" % k])
+    act(T.t1[:], T.t1[:], F.Identity, ["t1"], ["t1"], bias=1.0)
     for out, src, f, nm in ((T.im1[:], T.i1[:], -1.0, "im1"), (T.in2[:], T.i1[:], -2.0, "in2"),
                             (T.i64[:], T.i1[:], 64.0, "i64"), (T.i32[:], T.i1[:], 1.0, "i32"),
                             (T.im2[:], T.i1[:], -2048.0, "im2"), (T.im4[:], T.i1[:], -4096.0, "im4"),
+                            (T.i4[:], T.i1[:], 4096.0, "i4"),
                             (T.im8[:], T.i1[:], -8192.0, "im8"), (T.bo[:], T.bm[:], 128.0, "bo"),
                             (T.s8f[:], T.i1[:, 0:128:16], 1.0, "s8f"), (T.s8b[:], T.i1[:, 0:128:16], 2048.0, "s8b")):
         act(out, src, F.Identity, ["i1", "bm"], [nm], scale=f)
-    act(T.t1[:], T.t1[:], F.Identity, ["t1"], ["t1"], bias=1.0)
-    ts(T.i37[:], j, c(P), 37.0, A.is_equal, A.mult, ["jfa", "c0"], ["i37"])
+    ts(T.half[:], T.jh[:], 0.0, -1023.5, A.mult, A.add, ["jh"], ["half"])
+    ts(T.kmask[:], T.r16[:], c(U), 2.0 ** 15, A.not_equal, A.mult, ["r16", "c0"], ["kmask"])
+    ts(T.kpat[:], T.r16[:], 0.0, 2.0 ** 22, A.is_equal, A.mult, ["r16"], ["kpat"])
     ts(T.i16[:], j, c(P), None, A.is_equal, None, ["jfa", "c0"], ["i16"])
     ts(T.ones[:], T.j16[:], c(GB), None, A.is_equal, None, ["j16", "c0"], ["ones"])
-    ts(T.on2[:], T.j16[:], c(GB), -2.0, A.is_equal, A.mult, ["j16", "c0"], ["on2"])
-    ts(T.qb[:, 0:128], j, c(P), -8192.0, A.is_gt, A.mult, ["jfa", "c0"], ["qbA", "qbZ"])
-    ts(T.wn[:, 0:128], j, c(P), 4096.0, A.is_equal, A.mult, ["jfa", "c0"], ["wn"])
-    cp(T.eo[:], T.eoi[:], ["eoia", "eoib"], ["eo"])
-    for t in range(NT):
-        ts(T.tags[:, L * t:L * t + L], T.dm[:], float(L * t - (960 if t < 5 else 959)), 1.0 / 2048, A.add, A.mult,
-           ["dmA", "dmZ"], ["tag%d" % t])
-        if t == 1:
-            tt(T.qb[:, 0:128], T.qb[:, 0:128], T.wn[:, 0:128], A.add, ["qbA", "wn"], ["qbA", "qbZ"])
-        if t == 3:
-            tt(T.dpat[:], T.t1[:], T.t2[:], A.add, ["t1", "t2"], ["dpat"])
-        if t == 5:
-            tt(T.lz[:], T.qb[:, 0:128], T.ones[:], A.mult, ["qbA", "ones"], ["lz"])
-        if t == 7:
-            ts(T.dpat[:, :, 32:50:17], T.dpat[:, :, 32:50:17], 4096.0, None, A.mult, None, ["dpat"], ["dpat"])
+    act(T.on2[:], T.ones[:], F.Identity, ["ones"], ["on2"], scale=-2.0)
+
+    def more():
+        ts(T.qb[:, 0:128], j, c(P), -8192.0, A.is_gt, A.mult, ["jfa", "c0"], ["qbA", "qbZ"])
+        tt(T.dpat[:], T.t1[:], T.t2[:], A.add, ["t1", "t2"], ["dpat"])
+        tt(T.qb[:, 0:128], T.qb[:, 0:128], T.i4[:], A.add, ["qbA", "i4"], ["qbA", "qbZ"])
+        ts(T.i37[:], j, c(P), 37.0, A.is_equal, A.mult, ["jfa", "c0"], ["i37"])
+
+    def tag(t):
+        ts(T.tags[:, L * t:L * t + L], T.jh[:], float(L * t - (960 if t < 5 else 959)), 1.0 / 2048, A.add, A.mult,
+           ["jh"], ["tag%d" % t])
+
+    def rest():
+        tt(T.lz[:], T.qb[:, 0:128], T.ones[:], A.mult, ["qbA", "ones"], ["lz"])
+        for k, (s, n) in enumerate(SEG):
+            ts(T.dpat[:, s + n:s + n + 1], T.dpat[:, s + n:s + n + 1], 4096.0, None, A.mult, None, ["dpat"],
+               ["dp%d" % k])
+            ts(T.dpat[:, s + n + 1:s + n + 2], T.dpat[:, s + n + 1:s + n + 2], -1.0, None, A.mult, None, ["dpat"],
+               ["dq%d" % k])
+        wrote["dpat"] = wrote["dq%d" % (NC - 1)]
+    tag(0)
 
     tabw = T.tab[:, SP:SP + V]
-    part = {"A": (0, NA), "Z": (NA, L)}
     bank = {"dA": "b0", "dZ": "b1", "kA": "b6", "kZ": "b7", "cA": "b3", "cZ": "b4", "uA": "b2", "uZ": "b5"}
+    for z in "XY":
+        bank["d" + z], bank["k" + z] = bank["dA"], bank["kA"]
+
+    def over(name, a, b):
+        return [name + z for z in KEYS if PART[z][0] < b and PART[z][1] > a]
 
     def step(nm, t):
         home = (rank - t) % NR
@@ -250,88 +289,105 @@ def rank_program(g, core, T, topo):
         last = t == NT - 1
         hand_on = last or rank != NR - 1
         kt = t % NR if rank == 0 else t
-        kl, kbn, mkn = T.kb[:, 32 * kt:32 * kt + 12], ["kA%d" % kt, "kZ%d" % kt], "mk%d" % t
+        kl, kbn, mkn = T.kb[:, 32 * kt:32 * kt + 12], ["k%s%d" % (y, kt) for y in KEYS], "mk%d" % t
         arn = own if home == rank else ["ra%d" % home, "rb%d" % home]
         mo, mk = T.mko[:, L * t:L * t + L], T.mkb[:, t]
         recw = T.recs[:, 0:min(R + t * V, 2 * R)]
         recn = ["recs", "rece", "recf"][:t + 1]
         z = nm[-1]
-        a, b = part.get(z, (0, L))
-        sl, ca, cb, pa, pb = slice(a, b), a // 16, b // 16, a // 32, b // 32
+        a, b = PART.get(z, (0, L))
+        sl, ca, cb, pa, pb = slice(a, b), a // 16, b // 16, a // CL, b // CL
         if nm[:4] == "cand":
             src = T.chi[:, 0:V] if t == 0 else tabw
             cp(T.cand[:, sl], src.indirect(T.kb[:, 32 * kt + ca:32 * kt + cb]),
                ["chi" if t == 0 else "tab", "k%s%d" % (z, kt)], [nm])
-            if t == 0 and z == "A":
-                H = V // 2
-                for h in range(2):
-                    ts(T.tab[:, SP + V + h * H:SP + V + (h + 1) * H], T.chi[:, h * H:(h + 1) * H], float(R), None,
-                       A.add, None, ["chi"], ["ch0%d" % h])
-                    act(T.tab[:, SP + h * H:SP + (h + 1) * H], T.tab[:, SP + V + h * H:SP + V + (h + 1) * H],
-                        F.Identity, ["ch0%d" % h], ["tab%d" % h], bias=-float(R))
-                wrote["tab"], wrote["ch0"] = wrote["tab1"], wrote["ch01"]
-                order("g", ["recs"], [])
-                forward(rank, 0, own)
-                forward(rank, 1, own)
-                dma("y", "lext", ["recs"], ["rece"], T.recs[:, R:R + V], T.rec[:, 0:V])
-            if t == 1 and z == "A":
-                dma("y", "lex2", ["candA"], ["recf"], T.recs[:, R + V:2 * R], T.rec[:, V:R])
-        elif nm == "xh":
-            act(T.xh[:, 0:16 * CUT[1]], recw.indirect(T.cand[:, 0:CUT[1]]), F.Copy, recn + ["candA"], ["xh"])
-        elif nm == "pv":
-            n = 16 * CUT[1]
-            mm("b2", [(T.b2[:, 0:n], T.im1[:], T.ar[:, home * W:home * W + n], ["im1"] + arn),
-                      (T.b2[:, 0:n], T.i1[:], T.xh[:, 0:n], ["i1", "xh"])])
-        elif nm == "s0":
-            act(T.df[:, 0:16 * CUT[1]], T.b2[:, 0:16 * CUT[1]], F.Abs, ["b2"], ["df0"])
-        elif nm[0] in "vs" and nm[1:].isdigit():
+        elif nm == "init":
+            H = V // 2
+            cp(T.tab[:, SP:SP + H], T.chi[:, 0:H], ["chi"], ["tab0"])
+            cp(T.tab[:, SP + H:SP + V], T.chi[:, H:V], ["chi"], ["tab"])
+            act(T.tab[:, SP + V:SP + V + H], T.tab[:, SP:SP + H], F.Copy, ["tab0"], ["ch1"])
+            act(T.tab[:, SP + V + H:SP + 2 * V], T.tab[:, SP + H:SP + V], F.Copy, ["tab"], ["ch0"])
+            order("g", ["recs"], [])
+            forward(rank, 0, own)
+            forward(rank, 1, own)
+            dma("y", "lext", ["recs"], ["rece"], T.recs[:, R:R + V], T.rec[:, 0:V])
+        elif nm == "more":
+            more()
+        elif nm == "rest":
+            rest()
+        elif nm == "tag":
+            if not last:
+                tag(t + 1)
+        elif nm == "thw":
+            cp(c(TH), T.thi[:, 0:1], ["thi"], ["th"])
+            cp(c(WT), T.wi[:, 0:1], ["wi"], ["wt"])
+        elif nm == "bw":
+            ts(T.bw[:], T.jf[:, 0:144], c(G15), c(WT), A.is_equal, A.mult, ["jfa", "g15", "wt"], ["bw"])
+            ts(T.bwr[:], T.j16[:], c(GB), c(WT), A.is_equal, A.mult, ["j16", "c0", "wt"], ["bwr"])
+        elif nm[0] in "vsxw" and nm[1:].isdigit():
             k = int(nm[1:])
             a, b = CUT[k], CUT[k + 1]
-            if nm[0] == "v":
-                tt(T.df[:, 16 * a:16 * b], recw.indirect(T.cand[:, a:b]), T.ar[:, home * W + 16 * a:home * W + 16 * b],
-                   A.subtract, recn + ["candA" if a < NA else "candZ"] + arn, ["df%d" % k])
+            df, ar, n = T.df[:, 16 * a:16 * b], T.ar[:, home * W + 16 * a:home * W + 16 * b], 16 * (b - a)
+            if home != rank:
+                arn = arn[a // (L // 2):(b - 1) // (L // 2) + 1]
+            if k in BY_S:
+                i = BY_S.index(k)
+                xh, pv = T.xh[:, 512 * i:512 * i + n], ("b2", "b1")[i]
+            if nm[0] == "x":
+                act(xh, recw.indirect(T.cand[:, a:b]), F.Copy, recn + over("cand", a, b), ["xh%d" % k])
+            elif nm[0] == "w":
+                mm(pv, [(T[pv][:, 0:n], T.im1[:], ar, ["im1"] + arn), (T[pv][:, 0:n], T.i1[:], xh, ["i1", "xh%d" % k])])
+            elif nm[0] == "v":
+                tt(df, recw.indirect(T.cand[:, a:b]), ar, A.subtract, recn + over("cand", a, b) + arn, ["df%d" % k])
+            elif k in BY_S:
+                act(df, T[pv][:, 0:n], F.Abs, [pv], ["df%d" % k])
             else:
-                act(T.df[:, 16 * a:16 * b], T.df[:, 16 * a:16 * b], F.Abs, ["df%d" % k], ["df%d" % k])
-        elif nm[0] == "d" and z.isdigit():
-            a, b = DCUT[int(z)], DCUT[int(z) + 1]
+                act(df, df, F.Abs, ["df%d" % k], ["df%d" % k])
+        elif nm[0] == "d" and len(nm) == 2:
             rd = ["bm"] + ["df%d" % k for k in range(len(CUT) - 1) if CUT[k] < b and CUT[k + 1] > a]
-            d = bank["dA" if a < NA else "dZ"]
+            d = bank[nm]
             mm(d, [(T[d][:, a:b], T.bm[:, 15 - i:143 - i], T.df[:, 16 * a + i:16 * b:16], rd) for i in range(16)])
         elif nm == "krow":
-            act(T.krow[:], T.jf[:, 0:V].indirect(T.kb[:, 32 * kt:32 * kt + 18]), F.Identity,
-                ["jfa", "jfb", "kE%d" % kt] + kbn, ["krow"], bias=float(SP))
-        elif nm == "kex":
-            if kt == t:
-                cp(T.kb[:, 32 * kt + 12:32 * kt + 18], T.kb[:, 32 * kt + 1:32 * kt + 12:2], kbn, ["kE%d" % kt])
+            act(T.krow[:], T.jf[:, 0:V].indirect(kl), F.Identity, ["jfa", "jfb"] + kbn, ["krow"], bias=float(SP))
+        elif nm == "keyh":
+            ts(T.keyh[:], kl, float(SP - 1024), None, A.add, None, kbn, ["keyh"])
         elif nm == "keyf":
             ts(T.keyf[:, 0:12], kl, float(SP), None, A.add, None, kbn, ["keyf"])
-            if t == 0:
-                cp(c(TH), T.thi[:, 0:1], ["thi"], ["th"])
-                cp(c(WT), T.wi[:, 0:1], ["wi"], ["wt"])
-                ts(T.bw[:], T.jf[:, 0:144], c(G15), c(WT), A.is_equal, A.mult, ["jfa", "g15", "wt"], ["bw"])
-        elif nm == "eq":
-            tt(T.ne[:], T.keyf[:, 0:16].indirect(T.eo[:]), T.krow[:], A.not_equal, ["keyf", "eo", "krow"], ["ne"])
+        elif nm[:2] == "ne":
+            p = int(z)
+            for k, (s, n) in enumerate(SEG):
+                ts(T.ne[:, p, s:s + n], T.krow[:, CL * (p + 1) - n:CL * (p + 1)], T.keyf[:, NC * p + k:NC * p + k + 1],
+                   None, A.not_equal, None, ["keyf", "krow", "ne"], ["ne%d%d" % (p, k)])
         elif nm == "pl":
             if not fresh:
-                mm("b6", [(T.b6[:, 32:44], T.i32[:], T.keyf[:, 0:12], ["i32", "keyf"])]
-                   + [(T.b6[:, 32:44], T.bo[:, 15 - u:143 - u], T.mkb[:, t, :, u:32:16], ["bo", mkn])
+                mm("b6", [(T.b6[:, 32:44], T.i16[:], T.keyh[:], ["i16", "keyh"])]
+                   + [(T.b6[:, 32:44], T.bo[:, 15 - u:143 - u], T.mkb[:, t, :, u:CL:16], ["bo", mkn])
                       for u in range(16)])
-        elif nm == "o2":
+            if t == 1:
+                dma("y", "lex2", ["keyh"] if fresh else [mkn], ["recf"], T.recs[:, R + V:2 * R], T.rec[:, V:R])
+        elif nm == "o1":
             if not fresh:
-                ts(T.o2[:], T.b6[:, 32:44], -float(SP), None, A.add, None, ["b6"], ["o2"])
+                ts(T.o2[:, 16 * t:16 * t + 12], T.b6[:, 32:44], 1024.0 - SP, None, A.add, None, ["b6"], ["ob%d" % t])
         elif nm == "r1":
             if fresh:
-                act(T.r1[:], tabw.indirect(kl), F.Identity, ["tab"] + kbn, ["r1"], bias=MAGIC)
+                act(T.r1[:], tabw.indirect(kl), F.Identity, ["tab", "tab0"] + kbn, ["r1"], bias=MAGIC)
             else:
-                act(T.r1[:], T.tab[:, SP:SP + 2 * V].indirect(T.o2[:]), F.Identity, ["tab", "ch0", "o2"], ["r1"],
-                    bias=MAGIC)
+                act(T.r1[:], T.tab[:, SP:SP + 2 * V].indirect(T.o2[:, 16 * t:16 * t + 12]), F.Identity,
+                    ["tab", "ch0", "ch1", "ob%d" % t], ["r1"], bias=MAGIC)
+        elif nm == "cv":
+            if fresh:
+                ts(T.c1[:], tabw.indirect(kl), MAGIC, -MAGIC, A.add, A.add, ["tab", "tab0"] + kbn, ["c1"])
+            else:
+                ts(T.c1[:], T.tab[:, SP:SP + 2 * V].indirect(T.o2[:, 16 * t:16 * t + 12]), MAGIC, -MAGIC, A.add, A.add,
+                   ["tab", "ch0", "ob%d" % t], ["c1"])
         elif nm == "c1":
             act(T.c1[:], T.r1[:], F.Identity, ["r1"], ["c1"], bias=-MAGIC)
         elif nm == "wf":
-            ts(T.wf[:], T.cand[:], 4095.5, None, A.is_gt, None, ["candA", "candZ"], ["wf"])
+            ts(T.wf[:], T.cand[:], 4095.5, None, A.is_gt, None, over("cand", 0, L), ["wf"])
         elif nm == "py":
             mm("b7", [(T.b7[:, 256:256 + L], T.i16[:], T.tags[:, L * t:L * t + L], ["i16", "tag%d" % t]),
-                      (T.b7[:, 256:256 + L], T.im4[:], T.wf[:], ["im4", "wf"])])
+                      (T.b7[:, 256:256 + L], T.im4[:], T.wf[:], ["im4", "wf"])]
+               + ([] if fresh else [(T.b7[:, 256:256 + L], T.i4[:], mk, ["i4", mkn])]))
         elif nm == "yv":
             tt(T.yv[:], T.b7[:, 256:256 + L], T.c1[:], A.add, ["b7", "c1"], ["yv"])
         elif nm[:2] == "dm":
@@ -344,17 +400,17 @@ def rank_program(g, core, T, topo):
                 bias=155.0 - 1022.5 / 2048)
         elif nm[:2] in ("pc", "pu") or nm[:3] == "pre":
             pc, pu, n = T[bank["c" + z]], T[bank["u" + z]][:, sl], pb - pa
-            early = {"c": [(pc[:, 0:n, 0:50], T.i64[:], T.zero[:, 0:50 * n], ["i64", "zero"]),
-                           (pc[:, 0:n, 0:32], T.i64[:], T.ne[:, sl], ["i64", "ne"]),
-                           (pc[:, 0:n, 33:49], T.i64[:], T.ne[:, L + 16 * pa:L + 16 * pb], ["i64", "ne"]),
-                           (pc[:, 0:n, 32:50:17], T.i32[:], T.keyf[:, ca:cb], ["i32", "keyf"])], "u": []}
+            nes = ["ne%d%d" % (p, k) for p in range(pa, pb) for k in range(NC)] + ["nd%d" % k for k in range(NC)]
+            early = {"c": [(pc[:, 0:n, 0:SL], T.i64[:], T.ne[:, pa:pb], ["i64"] + nes)]
+                     + [(pc[:, 0:n, s + m], T.i16[:], T.keyh[:, pa:pb, k], ["i16", "keyh"])
+                        for k, (s, m) in enumerate(SEG)], "u": []}
             if not fresh:
-                early["c"] += [(pc[:, 0:n, 0:32], T.in2[:], T.mkb[:, t, pa:pb], ["in2", mkn]),
-                               (pc[:, 0:n, 33:49], T.in2[:], T.mkb[:, t, pa:pb, 16:32], ["in2", mkn])]
+                early["c"] += [(pc[:, 0:n, s:s + m], T.in2[:], T.mkb[:, t, pa:pb, CL - m:CL], ["in2", mkn])
+                               for s, m in SEG]
                 early["u"] += [(pu, T.im8[:], T.mkb[:, t, pa:pb], ["im8", mkn])]
-            late = {"c": [(pc[:, 0:n, 0:32], T.on2[:], T.fl[:, pa:pb], ["on2", "fl" + z]),
-                          (pc[:, 0:n, 33:49], T.on2[:], T.fl[:, pa:pb, 16:32], ["on2", "fl" + z])],
-                    "u": [(pu, T.lz[:], T.fl[:, pa:pb], ["lz", "fl" + z]), (pu, T.i37[:], T.dm[:, sl], ["i37", "dm" + z]),
+            late = {"c": [(pc[:, 0:n, s:s + m], T.on2[:], T.fl[:, pa:pb, CL - m:CL], ["on2", "fl" + z]) for s, m in SEG],
+                    "u": [(pu, T.lz[:], T.fl[:, pa:pb], ["lz", "fl" + z]),
+                          (pu, T.i37[:], T.dm[:, sl], ["i37"] + over("dm", a, b)),
                           (pu, T.im2[:], T.qb[:, sl], ["im2", "qb" + z])]}
             if nm[:3] == "pre":
                 for k in "cu":
@@ -368,38 +424,73 @@ def rank_program(g, core, T, topo):
         elif nm[:2] == "rr":
             for p in range(pa, pb):
                 op("v", ["dpat", bank["c" + z]], ["rr%d" % p],
-                   lambda e: e.tensor_tensor_scan(T.rr[:, p], T.dpat[:, 0], T[bank["c" + z]][:, p - pa, 0:50], 0.0,
-                                                  A.mult, A.min))
+                   lambda e: e.tensor_tensor_scan(T.rr[:, SL * p:SL * p + SL], T.dpat[:],
+                                                  T[bank["c" + z]][:, p - pa, 0:SL], 0.0, A.mult, A.min))
         elif nm[:3] == "off":
-            rd = ["rr%d" % p for p in range(pa, pb)]
-            ts(T.off[:, ca:cb:2], T.rr[:, pa:pb, 32], c(U), None, A.max, None, rd + ["c0"], [nm + "0"])
-            ts(T.off[:, ca + 1:cb:2], T.rr[:, pa:pb, 49], c(D1), None, A.max, None, rd + ["d1"], [nm + "1"])
+            o = 16 * (z == "Z")
+            ts(T.off[:, o:o + 16], T.rr[:, 0:L // CL * SL].indirect(T.ends[:, 0:1]), -1.0, None, A.mult, None,
+               ["rr%d" % p for p in range(L // CL)] + ["ends"], [nm])
         elif nm[:2] == "sc":
             p = int(z)
-            y = "A" if 32 * p < NA else "Z"
-            tt(T.tab[:, 0:SP + V].indirect(T.off[:, 2 * p:2 * p + 2]), T.yv[:, 32 * p:32 * p + 32],
-               T.ef[:, 32 * p:32 * p + 32], A.add, ["off%s0" % y, "off%s1" % y, "yv", "ef" + y], ["tab", "spare"])
-        elif nm == "fwd":
-            ahead = (rank - t) % NR
+            y = "A" if CL * p < PART["Z"][0] else "Z"
+            o = 16 * (y == "Z") + NC * p
+            tt(T.tab[:, 0:SP + V].indirect(T.off[:, o:o + NC]), T.yv[:, CL * p:CL * p + CL],
+               T.ef[:, CL * p:CL * p + CL], A.add, ["off" + y, "yv", "ef" + y],
+               ["tab", "spare"] + (["tab0"] if t == 0 else []))
+        elif nm[:2] == "fw":
             if 0 < t < NR - 1:
-                forward(ahead, 0, ["ra%d" % ahead])
-                forward(ahead, 1, ["rb%d" % ahead])
+                forward(home, "ab".index(z), ["r%s%d" % (z, home)])
         elif not hand_on:
             pass
+        elif nm[:2] == "pr":
+            pk = T[bank["k" + z]][:, 64 + a:64 + b]
+            mm(bank["k" + z], [(pk, T.i64[:], T.kmask[:, sl], ["i64", "kmask"]),
+                               (pk, T.i16[:], T.half[:, sl], ["i16", "half"]),
+                               (pk, T.bwr[:], T.dm[:, sl], ["bwr", "dm" + z])])
+        elif nm[:2] == "ks":
+            op("v", ["kpat", bank["k" + z]], [nm],
+               lambda e: e.tensor_tensor_scan(T.kx[:, sl], T.kpat[:, sl], T[bank["k" + z]][:, 64 + a:64 + b], 0.0,
+                                              A.add, A.min))
+        elif nm[:2] == "kr" and "ks" + z in ORDER.split():
+            ts(T.kr[:, ca:cb], T.kx[:, a + 15:b:16], MAGIC * V, -MAGIC * V, A.add, A.add, ["ks" + z], [nm])
+        elif nm[:2] == "kf" and "ks" + z in ORDER.split():
+            tt(T.kf[:, ca:cb], T.kx[:, a + 15:b:16], T.kr[:, ca:cb], A.subtract, ["ks" + z, "kr" + z], [nm])
         elif nm[:2] == "pk":
-            mm(bank[nm[1:]], [(T[bank[nm[1:]]][:, ca:cb], T.bw[:, 15 - u:143 - u], T.dm[:, a + u:b:16], ["bw", "dm" + z])
-                              for u in range(16)])
-        elif nm[:2] == "ki":
-            cp(T.ki[:, ca:cb], T[bank["k" + z]][:, ca:cb], [bank["k" + z]], [nm])
-        elif nm[:2] == "kj":
-            ts(T.kj[:, ca:cb], T.ki[:, ca:cb], V - 1, None, A.bitwise_and, None, ["ki" + z], [nm])
+            pk = T[bank[nm[1:]]][:, ca:cb]
+            mm(bank[nm[1:]], [(pk, T.i16[:], T.half[:, ca:cb], ["i16", "half"])]
+               + [(pk, T.bw[:, 15 - u:143 - u], T.dm[:, a + u:b:16], ["bw", "dm" + z]) for u in range(16)])
+        elif nm[:2] == "kr":
+            ts(T.kr[:, ca:cb], T[bank["k" + z]][:, ca:cb], MAGIC * V, -MAGIC * V, A.add, A.add, [bank["k" + z]], [nm])
+        elif nm[:2] == "kf":
+            tt(T.kf[:, ca:cb], T[bank["k" + z]][:, ca:cb], T.kr[:, ca:cb], A.subtract, [bank["k" + z], "kr" + z], [nm])
         elif nm[:2] == "ko":
             o = T.ko[:, 16 * t + ca:16 * t + cb]
-            cp(o, T.kj[:, ca:cb], ["kj" + z], ["o%s%d" % (z, t)])
+            ts(o, T.kf[:, ca:cb], 1023.5, None, A.add, None, ["kf" + z], ["o%s%d" % (z, t)])
             if not last:
                 send(nxt, "k%s%d" % (z, t + 1), ["o%s%d" % (z, t)], T.kb[:, 32 * (t + 1) + ca:32 * (t + 1) + cb], o)
+        elif nm[:2] == "va":
+            v = T.b0[:, 256 + a:256 + b]
+            mm("b0", ([] if fresh else [(v, T.im8[:], T.mkb[:, t, pa:pb], ["im8", mkn])])
+               + [(v, T.i32[:], T.yv[:, sl], ["i32", "yv"]), (v, T.i32[:], T.ef[:, sl], ["i32", "ef" + z])])
+        elif nm[:2] == "vb":
+            act(T.val[:, sl], T.b0[:, 256 + a:256 + b], F.Copy, ["b0"], [nm])
         elif nm == "wn":
-            tt(T.wn[:], tabw.indirect(kl), T.yv[:], A.is_equal, ["tab", "yv"] + kbn, ["wn"])
+            if LIST:
+                tt(T.wn[:], tabw.indirect(kl), T.val[:], A.is_equal, ["tab", "vbA", "vbZ"] + kbn, ["wn"])
+            else:
+                tt(T.wn[:], tabw.indirect(kl), T.yv[:], A.is_equal, ["tab", "yv"] + kbn, ["wn"])
+        elif nm in ("poE", "poL"):
+            po = T.b6[:, 32:44]
+            if nm == "poL" and not last:
+                mm("b6", [(po, T.bo[:, 15 - u:143 - u], T.wn[:, u:L:16], ["bo", "wn"]) for u in range(16)], False, True)
+            elif not last:
+                mm("b6", [(po, T.i32[:], T.kf[:], ["i32"] + over("kf", 0, L))]
+                   + [(po, T.bo[:, 15 - u:143 - u], T.mkb[:, t, :, u:CL:16], ["bo", mkn])
+                      for u in range(0 if fresh else 16)], True, False)
+        elif nm == "o2":
+            o = T.o2o[:, 16 * t:16 * t + 12]
+            ts(o, T.b6[:, 32:44], 1023.5, None, A.add, None, ["b6"], ["oo%d" % t])
+            send(nxt, "oa%d" % (t + 1), ["oo%d" % t], T.o2[:, 16 * (t + 1):16 * (t + 1) + 12], o)
         elif nm == "pm":
             mm("b5", ([] if fresh else [(T.b5[:, 256:256 + L], T.i1[:], mk, ["i1", mkn])])
                + [(T.b5[:, 256:256 + L], T.ones[:], T.wn[:], ["ones", "wn"])])
@@ -411,45 +502,64 @@ def rank_program(g, core, T, topo):
             raise ValueError(nm)
 
     for t in range(NT):
-        for nm in ORDER.split():
+        names = ORDER.split()
+        if t == 0:
+            early = EARLY.split()
+            names = early + [nm for nm in names if nm not in early]
+        for nm in names:
             if nm[0] != "<":
                 step(nm, t)
             elif t > 0:
                 step(nm[1:], t - 1)
-            if nm == "<mo":
-                step("fwd", t)
 
     t = NT - 1
     banks = ["b1", "b2", "b6", "b7", "b1"]
-    cut = [0, 256, 768, 1280, 1792, 2048]
-    act(T.r1[:], T.jf[:, 0:V].indirect(T.ko[:, 16 * t:16 * t + 12]), F.Identity,
-        ["jfa", "jfb", "oA%d" % t, "oZ%d" % t], ["r1"])
-    step("wn", t)
-    act(T.c1[:], T.r1[:, 0:L].indirect(T.rv[:]), F.Identity, ["r1", "rv"], ["c1"])
-    mm("b0", [(T.b0[0:8, 0:L], T.s8f[:], T.c1[:], ["s8f", "c1"])], True, False)
-    step("pm", t)
+    cut = [0, 192, 704, 1216, 1728, 2048]
+
+    by_s = (2, 4)
+    act(T.one[:], T.jf[:, 0:512], F.Identity, ["jfa", "jfb"], ["one"], scale=0.0, bias=1.0)
+    act(T.imm[:], T.i1[:], F.Identity, ["i1"], ["imm"], scale=-MAGIC)
 
     def sign(k):
         a, b = cut[k], cut[k + 1]
+        o = T[banks[k]][:, 0:b - a]
         act(T.so[:, a:b], T.tab[:, SP + a:SP + b], F.Sign, ["tab"], ["so%d" % k], bias=-4095.5)
-        mm(banks[k], [(T[banks[k]][:, 0:b - a], T.im2[:], T.so[:, a:b], ["im2", "so%d" % k])])
-    for k in range(4):
-        sign(k)
-    for k in range(6):
-        if k < 5:
-            a, b = cut[k], cut[k + 1]
-            ts(T.ro[:, a:b], T.tab[:, SP + a:SP + b], MAGIC, -(MAGIC + 2048.0), A.add, A.add, ["tab"], ["ro%d" % k])
-        if k > 0:
-            a, b = cut[k - 1], cut[k]
-            tt(T.oc[:, a:b], T[banks[k - 1]][:, 0:b - a], T.ro[:, a:b], A.add, [banks[k - 1], "ro%d" % (k - 1)],
-               ["oc%d" % k])
-            dma("y", "stored", ["oc%d" % k], [], T.yc[:, a:b], T.oc[:, a:b])
-        if k == 1:
-            sign(4)
-            step("mo", t)
-            act(T.qb[:], T.mko[:, L * t:L * t + L].indirect(T.rv[:]), F.Copy, ["mo%d" % t, "rv"], ["qbA", "qbZ"])
-            mm("b0", [(T.b0[0:8, 0:L], T.s8b[:], T.qb[:], ["s8b", "qbA"])], False, True)
-            act(T.yks[0:8, :], T.b0[0:8, 0:L], F.Copy, ["b0"], ["yks"])
-            dma("s", "stored", ["yks"], [], T.yk[:], T.yks[0:8, :])
+        less = []
+        if k in by_s:
+            act(T.ro[:, a:b], T.tab[:, SP + a:SP + b], F.Identity, ["tab"], ["ro%d" % k], bias=MAGIC)
+            less = [(o, T.imm[:], T.one[:, 0:b - a], ["imm", "one"]), (o, T.im2[:], T.one[:, 0:b - a], ["im2", "one"])]
+        mm(banks[k], less + [(o, T.im2[:], T.so[:, a:b], ["im2", "so%d" % k])])
+
+    def block(k):
+        a, b = cut[k], cut[k + 1]
+        ts(T.ro[:, a:b], T.tab[:, SP + a:SP + b], MAGIC, -(MAGIC + 2048.0), A.add, A.add, ["tab"], ["ro%d" % k])
+
+    def store(k):
+        a, b = cut[k], cut[k + 1]
+        tt(T.oc[:, a:b], T[banks[k]][:, 0:b - a], T.ro[:, a:b], A.add, [banks[k], "ro%d" % k], ["oc%d" % k])
+        dma("y", "stored", ["oc%d" % k], [], T.yc[:, a:b], T.oc[:, a:b])
+    sign(0)
+    sign(1)
+    block(0)
+    block(1)
+    store(0)
+    step("wn", t)
+    sign(2)
+    step("pm", t)
+    sign(3)
+    store(1)
+    block(3)
+    store(2)
+    step("mo", t)
+    sign(4)
+    act(T.r1[:], T.jf[:, 0:V].indirect(T.ko[:, 16 * t:16 * t + 12]), F.Identity,
+        ["jfa", "jfb"] + ["o%s%d" % (z, t) for z in KEYS], ["r1"])
+    act(T.qb[:], T.mko[:, L * t:L * t + L].indirect(T.rv[:]), F.Copy, ["mo%d" % t, "rv"], ["qbA", "qbZ"])
+    store(3)
+    store(4)
+    cp(T.c1[:], T.r1[:, 0:L].indirect(T.rv[:]), ["r1", "rv"], ["c1"])
+    mm("b0", [(T.b0[0:8, 0:L], T.s8b[:], T.qb[:], ["s8b", "qbA"]), (T.b0[0:8, 0:L], T.s8f[:], T.c1[:], ["s8f", "c1"])])
+    act(T.yks[0:8, :], T.b0[0:8, 0:L], F.Copy, ["b0"], ["yks"])
+    dma("s", "stored", ["yks"], [], T.yk[:], T.yks[0:8, :])
     for sem, n in count.items():
         g.wait_ge(T.sem[sem], n)

from concourse.mybir import AluOpType, ActivationFunctionType

NR, NT, L, V, R = 8, 10, 192, 2048, 4096
NC = 4
CL = 16 * NC
SP = CL
SEG = [(k * (CL + 2) - 8 * k * (k - 1), CL - 16 * k) for k in range(NC)]
SL = SEG[-1][0] + 18
CUT = [0, 30, 64, 96, 128, 160, 180, 192]
BY_S = [0]
PART = {"X": (0, 64), "Y": (64, 128), "A": (0, 128), "Z": (128, 192)}
KEYS = "AZ"
LIST = False
EARLY = ("candA candZ keyh keyf init krow more x0 wf v1 thw w0 py v2 s1 s0 bw dX v3 s2 v4 s3 dY v5 r1 s4 v6 ne0 ne1 "
         "preA dmA flA prA pcA rest s5 s6 dZ qbA c1 ksA rrA puA ne2 preZ krA flZ dmZ yv kfA offA efA pcZ koA sc0 rrZ "
         "prZ ksZ qbZ sc1 krZ puZ efZ offZ kfZ sc2 koZ tag")
MAGIC = 12582912.0
ORDER = ("candA <wn x0 <pm w0 v2 <mo v3 fwa candZ s2 keyf s3 keyh v1 s0 krow s1 wf dY pl v4 s4 ne1 py dX ne0 o1 v5 v6 "
         "dmA fwb r1 flA ne2 preA prA s5 ksA pcA rrA s6 qbA krA dZ puA c1 yv preZ efA kfA dmZ flZ offA pcZ koA sc0 "
         "rrZ prZ qbZ ksZ sc1 krZ offZ puZ efZ kfZ sc2 koZ tag")

BF, F32, F16, I32, U16 = "bfloat16", "float32", "float16", "int32", "uint16"
SCRATCH = {name: ("sbuf", [128] + shape, dtype) for name, shape, dtype in [
    ("chi", [V], I32), ("recs", [2 * R], BF), ("tab", [SP + 2 * V], F32),
    ("ats", [L], BF), ("atr", [L], BF), ("ar", [NR * 16 * L], BF), ("df", [16 * L], BF), ("xh", [1024], BF),
    ("k0i", [12], I32), ("k0h", [12], F16), ("thi", [4], I32), ("wi", [4], I32),
    ("kb", [NT * 32], U16), ("ko", [NT * 16], U16), ("mkb", [NT, L // CL, CL], BF), ("mko", [NT * L], BF),
    ("jf", [V], F32), ("j16", [128], F32), ("rel", [SL], BF), ("t1", [SL], BF), ("t2", [SL], BF),
    ("pi", [8], I32), ("col", [24], F32), ("ends", [2], U16), ("rv", [12], U16),
    ("bm", [144], BF), ("bw", [144], F16), ("bo", [144], BF), ("i1", [128], BF), ("im1", [128], BF),
    ("in2", [128], BF), ("i64", [128], BF), ("i32", [128], F32), ("i16", [128], F16), ("i37", [128], F16),
    ("im2", [128], BF), ("im4", [128], BF), ("i4", [128], BF), ("imm", [128], BF), ("one", [512], BF),
    ("im8", [128], BF), ("ones", [128], BF), ("on2", [128], BF),
    ("lz", [128], BF), ("prv", [128], F16), ("s8f", [8], F32), ("s8b", [8], BF),
    ("tags", [NT * L], F16), ("dpat", [SL], BF),
    ("cand", [L], U16), ("keyf", [12], F32), ("keyh", [L // CL, NC], F16), ("krow", [L], F32),
    ("ne", [L // CL, SL], BF), ("rr", [L // CL * SL], F32), ("off", [32], U16),
    ("o2", [NT * 16], U16), ("o2o", [NT * 16], U16), ("val", [L], F32), ("r1", [L], F32), ("c1", [L], F32),
    ("wf", [L], BF), ("yv", [L], F32),
    ("ef", [L], F32), ("dm", [L], F16), ("fl", [L // CL, CL], BF), ("qb", [L], BF), ("wn", [L], BF),
    ("kr", [12], F32), ("kf", [12], F32), ("half", [L], F16), ("jh", [L], F16),
    ("kx", [L], F32), ("kpat", [L], BF), ("kmask", [L], BF), ("r16", [L], BF), ("bwr", [128], F16),
    ("ro", [V], F32), ("so", [V], BF), ("oc", [V], F32), ("yks", [L], F32)]}
PSUM = ("b0", "b1", "b2", "b3", "b4", "b5", "b6", "b7")
for _b in PSUM:
    SCRATCH[_b] = ("psum", [128, 32 // NC ** 2, 16 * NC ** 2] if _b in ("b3", "b4") else [128, 512], F32)
SEMAPHORES = (["qv", "qs", "qp", "qg", "sent", "lsm", "lch", "lrec", "lext", "lex2", "lk0", "lat", "stored"]
              + ["k%s%d" % (z, t) for t in range(NT) for z in PART]
              + ["%s%d" % (z, t) for t in range(NT) for z in ("ma", "oa")]
              + ["aa%d" % h for h in range(NR)] + ["ab%d" % h for h in range(NR)])

A = AluOpType
F = ActivationFunctionType


def rank_program(g, core, T, topo):
    rank = T.rank_of(core)
    if rank is None:
        return
    eng = {"v": g.vector, "s": g.scalar, "p": g.tensor, "g": g, "y": g.sync}
    qsem = {"v": "qv", "s": "qs", "p": "qp", "g": "qg"}
    count = {}
    know = {q: {} for q in eng}
    snap = {}
    wrote, read = {}, {}

    def need(q, ev):
        sem, n = ev
        if know[q].get(sem, 0) >= n:
            return
        eng[q].wait_ge(T.sem[sem], n)
        know[q][sem] = n
        for s, m in snap.get(ev, {}).items():
            if know[q].get(s, 0) < m:
                know[q][s] = m

    def order(q, rd, wr):
        evs = {}
        for b in rd:
            if b in wrote:
                evs[wrote[b][0]] = max(evs.get(wrote[b][0], 0), wrote[b][1])
        for b in wr:
            free = qsem.get(q) if b in PSUM else None
            if b in wrote and wrote[b][0] != free:
                evs[wrote[b][0]] = max(evs.get(wrote[b][0], 0), wrote[b][1])
            for s, n in read.get(b, {}).items():
                evs[s] = max(evs.get(s, 0), n)
        for ev in sorted(evs.items(), key=lambda e: e[0] == qsem.get(q)):
            need(q, ev)

    def note(ev, q, rd, wr):
        snap[ev] = dict(know[q])
        for b in rd:
            read.setdefault(b, {})[ev[0]] = ev[1]
        for b in wr:
            wrote[b] = ev
            read[b] = {}

    def op(q, rd, wr, call):
        wr = list(wr) + [b for b in rd if b in PSUM]
        rd = [b for b in rd if b not in PSUM]
        order(q, rd, wr)
        sem = qsem[q]
        count[sem] = count.get(sem, 0) + 1
        call(eng[q]).then_inc(T.sem[sem], 1)
        note((sem, count[sem]), q, rd, wr)

    def dma(q, sem, rd, wr, out, in_, **kw):
        order(q, rd, wr)
        count[sem] = count.get(sem, 0) + 16
        eng[q].dma_start(out, in_, **kw).then_inc(T.sem[sem], 16)
        note((sem, count[sem]), q, rd, wr)

    def send(to, sem, rd, out, in_):
        order("g", rd, [])
        dst = T.cores[to]
        rid, pid, _ = topo.addr(dst)
        g.remote_dma(out, in_, T.sem[sem], T.sem.sent, pid, rid, topo.mask(core, dst))
        count["sent"] = count.get("sent", 0) + len(topo.engines(core, dst))

    def lands(frm, sem, *regions):
        count[sem] = len(topo.engines(T.cores[frm], core))
        for b in regions:
            wrote[b] = (sem, count[sem])

    def ts(out, in0, s1, s2, o0, o1, rd, wr):
        if o1 is None:
            op("v", rd, wr, lambda e: e.tensor_scalar(out, in0, s1, None, o0))
        else:
            op("v", rd, wr, lambda e: e.tensor_scalar(out, in0, s1, s2, o0, o1))

    def tt(out, a, b, o, rd, wr):
        op("v", rd, wr, lambda e: e.tensor_tensor(out, a, b, o))

    def cp(out, in_, rd, wr):
        op("v", rd, wr, lambda e: e.tensor_copy(out, in_))

    def fill(out, x, rd, wr):
        op("v", rd, wr, lambda e: e.memset(out, x))

    def act(out, in_, f, rd, wr, **kw):
        op("s", rd, wr, lambda e: e.activation(out, in_, f, **kw))

    def mm(bank, terms, first=True, final=True):
        for n, (out, lt, rhs, rd) in enumerate(terms):
            op("p", rd, [bank],
               lambda e: e.matmul(out, lt, rhs, first and n == 0, final and n == len(terms) - 1))

    def iota(out, pat, base, mul, wr, flt):
        if flt:
            op("g", [], wr, lambda e: e.iota(out, pat, base, mul, allow_small_or_imprecise_dtypes=True))
        else:
            op("g", [], wr, lambda e: e.iota(out, pat, base, mul))

    nxt, prv = (rank + 1) % NR, (rank - 1) % NR
    W = 16 * L

    def forward(h, k, rd):
        half = T.ar[:, h * W + k * W // 2:h * W + (k + 1) * W // 2]
        send(nxt, "a%s%d" % ("ab"[k], h), rd, half, half)

    for s in range(1, NR):
        for k in "ab":
            lands(prv, "a%s%d" % (k, (rank - s) % NR), "r%s%d" % (k, (rank - s) % NR))
    if rank == 0:
        for t in range(1, NR):
            lands((-t) % NR, "kZ%d" % t, *["k%s%d" % (z, t) for z in KEYS])
    else:
        for t in range(1, NT):
            for z in KEYS:
                lands(prv, "k%s%d" % (z, t), "k%s%d" % (z, t))
            lands(prv, "ma%d" % t, "mk%d" % t)
            if LIST:
                lands(prv, "oa%d" % t, "ob%d" % t)

    dma("s", "lat", [], ["ats"], T.ats[:], T.at[:])
    dma("y", "lk0", [], ["k0i"], T.k0i[:], T.key0[:])
    dma("y", "lch", [], ["chi"], T.chi[:], T.ch[:])
    dma("y", "lrec", [], ["recs"], T.recs[:, 0:R], T.rec[:])
    iota(T.pi[:, 0:1], [[0, 1]], 0, 1, ["pi0"], False)
    iota(T.jf[:, 0:192], [[1, 192]], 0, 0, ["jfa"], True)
    iota(T.j16[:], [[16, 8], [0, 16]], 0, 0, ["j16"], True)
    dma("g", "lsm", [], ["thi"], T.thi[:, 0:1], T.th[:], allow_slow_non_contiguous=True)
    dma("g", "lsm", [], ["wi"], T.wi[:, 0:1], T.w[:], allow_slow_non_contiguous=True)
    wrote["thi"] = wrote["wi"]
    for k, (s, n) in enumerate(SEG):
        iota(T.rel[:, s:s + n + 2], [[1, n + 2]], 0, 0, ["rel%d" % k], True)
    iota(T.r16[:], [[0, 12], [1, 16]], 0, 0, ["r16"], True)
    iota(T.jf[:, 192:V], [[1, V - 192]], 192, 0, ["jfb"], True)

    def c(k):
        return T.col[:, k:k + 1]
    P, GB, U, KK, KQ, G15, U1, TH, WT, EB, RV, UR, X0, X1, X2 = range(15)
    j = T.jf[:, 0:128]
    ts(T.pi[:, 1:2], T.pi[:, 0:1], 112, None, A.bitwise_and, None, ["pi0"], ["pi1"])
    ts(T.pi[:, 2:3], T.pi[:, 0:1], 15, None, A.bitwise_and, None, ["pi0"], ["pi2"])
    ts(T.pi[:, 3:4], T.pi[:, 0:1], NC - 1, None, A.bitwise_and, None, ["pi0"], ["pi3"])
    ts(T.pi[:, 4:5], T.pi[:, 0:1], 16 - NC, None, A.bitwise_and, None, ["pi0"], ["pi4"])
    fill(T.tab[:, 0:SP], 0.0, [], ["spare"])
    cp(T.col[:, 0:5], T.pi[:, 0:5], ["pi0", "pi1", "pi2", "pi3", "pi4"], ["c0"])
    cp(T.jh[:], T.jf[:, 0:L], ["jfa"], ["jh"])
    for p in range(L // CL):
        act(T.ne[:, p], T.jf[:, 0:SL], F.Identity, ["jfa"], ["ne"], scale=0.0, bias=16.0)
        act(T.rr[:, SL * p:SL * p + SL], T.jf[:, 0:SL], F.Identity, ["jfa"], ["rr%d" % p], scale=0.0)
    ts(c(UR), c(U), -1.0, 191.0, A.mult, A.add, ["c0"], ["ur"])
    ts(c(G15), c(GB), 15.0, None, A.add, None, ["c0"], ["g15"])
    ts(c(U1), c(U), 1.0, None, A.add, None, ["c0"], ["u1"])
    ts(c(X0), c(KK), 1.0, None, A.add, None, ["c0"], ["x0"])
    ts(c(X1), c(KK), -8.0, float(CL + 2), A.mult, A.add, ["c0"], ["x1"])
    ts(c(X2), c(KQ), SL / NC, -1.0, A.mult, A.add, ["c0"], ["x2"])
    ts(T.rv[:], T.jf[:, 0:12], -16.0, c(UR), A.mult, A.add, ["jfa", "ur"], ["rv"])
    ts(c(RV), c(G15), c(U), None, A.subtract, None, ["g15", "c0"], ["crv"])
    ts(c(EB), c(U), -256.0, float(1 + 2048 * 190 + 128), A.mult, A.add, ["c0"], ["eb"])
    ts(T.i1[:], j, c(P), None, A.is_equal, None, ["jfa", "c0"], ["i1"])

    cp(T.atr[:], T.ats[:, 0:L].indirect(T.rv[:]), ["ats", "rv"], ["atr"])
    ts(T.prv[:], j, c(RV), None, A.is_equal, None, ["jfa", "crv"], ["prv"])
    cp(T.k0h[:], T.k0i[:], ["k0i"], ["k0h"])
    ts(T.bm[:], T.jf[:, 0:144], c(G15), None, A.is_equal, None, ["jfa", "g15"], ["bm"])
    for k in range(12):
        mm("b6", [(T.b6[:, k:k + 1], T.prv[:], T.k0h[:, 11 - k:12 - k], ["prv", "k0h"])])
    for i in range(16):
        o = T.ar[:, rank * W + i:(rank + 1) * W:16]
        if i % 2 == 1:
            act(o, T.atr[:], F.Copy, ["atr"], ["own%d" % i])
        else:
            cp(o, T.atr[:], ["atr"], ["own%d" % i])
    own = ["own%d" % i for i in range(16)]
    cp(T.kb[:, 0:12], T.b6[:, 0:12], ["b6"], ["k%s0" % z for z in KEYS])
    if rank != 0:
        t0 = (-rank) % NR
        send(0, "kZ%d" % t0, ["kZ0"], T.kb[:, 32 * t0:32 * t0 + 12], T.kb[:, 0:12])

    ts(c(X0), c(X0), c(X1), c(X2), A.mult, A.add, ["x0", "x1", "x2"], ["x0"])
    for k, (s, n) in enumerate(SEG):
        ts(T.ne[:, :, s + n + 1], T.jf[:, 0:L // CL], 0.0, c(U), A.mult, A.add, ["jfa", "c0", "ne"], ["nd%d" % k])
    ts(T.ends[:, 0:1], c(X0), float(L // CL * SL - 1), None, A.min, None, ["x0"], ["ends"])
    rels = ["rel%d" % k for k in range(NC)]
    ts(T.t1[:], T.rel[:], c(U), -1.0, A.is_equal, A.mult, rels + ["c0"], ["t1"])
    ts(T.t2[:], T.rel[:], c(U1), -2.0, A.is_equal, A.mult, rels + ["u1"], ["t2"])
    for k, (s, n) in enumerate(SEG):
        ts(T.ne[:, :, s + n + 1], T.ne[:, :, s + n + 1], 16.0 * k, -1.0 / 64, A.add, A.mult, ["nd%d" % k], ["nd%d" % k])
    act(T.t1[:], T.t1[:], F.Identity, ["t1"], ["t1"], bias=1.0)
    for out, src, f, nm in ((T.im1[:], T.i1[:], -1.0, "im1"), (T.in2[:], T.i1[:], -2.0, "in2"),
                            (T.i64[:], T.i1[:], 64.0, "i64"), (T.i32[:], T.i1[:], 1.0, "i32"),
                            (T.im2[:], T.i1[:], -2048.0, "im2"), (T.im4[:], T.i1[:], -4096.0, "im4"),
                            (T.i4[:], T.i1[:], 4096.0, "i4"),
                            (T.im8[:], T.i1[:], -8192.0, "im8"), (T.bo[:], T.bm[:], 128.0, "bo"),
                            (T.s8f[:], T.i1[:, 0:128:16], 1.0, "s8f"), (T.s8b[:], T.i1[:, 0:128:16], 2048.0, "s8b")):
        act(out, src, F.Identity, ["i1", "bm"], [nm], scale=f)
    ts(T.half[:], T.jh[:], 0.0, -1023.5, A.mult, A.add, ["jh"], ["half"])
    ts(T.kmask[:], T.r16[:], c(U), 2.0 ** 15, A.not_equal, A.mult, ["r16", "c0"], ["kmask"])
    ts(T.kpat[:], T.r16[:], 0.0, 2.0 ** 22, A.is_equal, A.mult, ["r16"], ["kpat"])
    ts(T.i16[:], j, c(P), None, A.is_equal, None, ["jfa", "c0"], ["i16"])
    ts(T.ones[:], T.j16[:], c(GB), None, A.is_equal, None, ["j16", "c0"], ["ones"])
    act(T.on2[:], T.ones[:], F.Identity, ["ones"], ["on2"], scale=-2.0)

    def more():
        ts(T.qb[:, 0:128], j, c(P), -8192.0, A.is_gt, A.mult, ["jfa", "c0"], ["qbA", "qbZ"])
        tt(T.dpat[:], T.t1[:], T.t2[:], A.add, ["t1", "t2"], ["dpat"])
        tt(T.qb[:, 0:128], T.qb[:, 0:128], T.i4[:], A.add, ["qbA", "i4"], ["qbA", "qbZ"])
        ts(T.i37[:], j, c(P), 37.0, A.is_equal, A.mult, ["jfa", "c0"], ["i37"])

    def tag(t):
        ts(T.tags[:, L * t:L * t + L], T.jh[:], float(L * t - (960 if t < 5 else 959)), 1.0 / 2048, A.add, A.mult,
           ["jh"], ["tag%d" % t])

    def rest():
        tt(T.lz[:], T.qb[:, 0:128], T.ones[:], A.mult, ["qbA", "ones"], ["lz"])
        for k, (s, n) in enumerate(SEG):
            ts(T.dpat[:, s + n:s + n + 1], T.dpat[:, s + n:s + n + 1], 4096.0, None, A.mult, None, ["dpat"],
               ["dp%d" % k])
            ts(T.dpat[:, s + n + 1:s + n + 2], T.dpat[:, s + n + 1:s + n + 2], -1.0, None, A.mult, None, ["dpat"],
               ["dq%d" % k])
        wrote["dpat"] = wrote["dq%d" % (NC - 1)]
    tag(0)

    tabw = T.tab[:, SP:SP + V]
    bank = {"dA": "b0", "dZ": "b1", "kA": "b6", "kZ": "b7", "cA": "b3", "cZ": "b4", "uA": "b2", "uZ": "b5"}
    for z in "XY":
        bank["d" + z], bank["k" + z] = bank["dA"], bank["kA"]

    def over(name, a, b):
        return [name + z for z in KEYS if PART[z][0] < b and PART[z][1] > a]

    def step(nm, t):
        home = (rank - t) % NR
        fresh = t == 0 or rank == 0
        last = t == NT - 1
        hand_on = last or rank != NR - 1
        kt = t % NR if rank == 0 else t
        kl, kbn, mkn = T.kb[:, 32 * kt:32 * kt + 12], ["k%s%d" % (y, kt) for y in KEYS], "mk%d" % t
        arn = own if home == rank else ["ra%d" % home, "rb%d" % home]
        mo, mk = T.mko[:, L * t:L * t + L], T.mkb[:, t]
        recw = T.recs[:, 0:min(R + t * V, 2 * R)]
        recn = ["recs", "rece", "recf"][:t + 1]
        z = nm[-1]
        a, b = PART.get(z, (0, L))
        sl, ca, cb, pa, pb = slice(a, b), a // 16, b // 16, a // CL, b // CL
        if nm[:4] == "cand":
            src = T.chi[:, 0:V] if t == 0 else tabw
            cp(T.cand[:, sl], src.indirect(T.kb[:, 32 * kt + ca:32 * kt + cb]),
               ["chi" if t == 0 else "tab", "k%s%d" % (z, kt)], [nm])
        elif nm == "init":
            H = V // 2
            cp(T.tab[:, SP:SP + H], T.chi[:, 0:H], ["chi"], ["tab0"])
            cp(T.tab[:, SP + H:SP + V], T.chi[:, H:V], ["chi"], ["tab"])
            act(T.tab[:, SP + V:SP + V + H], T.tab[:, SP:SP + H], F.Copy, ["tab0"], ["ch1"])
            act(T.tab[:, SP + V + H:SP + 2 * V], T.tab[:, SP + H:SP + V], F.Copy, ["tab"], ["ch0"])
            order("g", ["recs"], [])
            forward(rank, 0, own)
            forward(rank, 1, own)
            dma("y", "lext", ["recs"], ["rece"], T.recs[:, R:R + V], T.rec[:, 0:V])
        elif nm == "more":
            more()
        elif nm == "rest":
            rest()
        elif nm == "tag":
            if not last:
                tag(t + 1)
        elif nm == "thw":
            cp(c(TH), T.thi[:, 0:1], ["thi"], ["th"])
            cp(c(WT), T.wi[:, 0:1], ["wi"], ["wt"])
        elif nm == "bw":
            ts(T.bw[:], T.jf[:, 0:144], c(G15), c(WT), A.is_equal, A.mult, ["jfa", "g15", "wt"], ["bw"])
            ts(T.bwr[:], T.j16[:], c(GB), c(WT), A.is_equal, A.mult, ["j16", "c0", "wt"], ["bwr"])
        elif nm[0] in "vsxw" and nm[1:].isdigit():
            k = int(nm[1:])
            a, b = CUT[k], CUT[k + 1]
            df, ar, n = T.df[:, 16 * a:16 * b], T.ar[:, home * W + 16 * a:home * W + 16 * b], 16 * (b - a)
            if home != rank:
                arn = arn[a // (L // 2):(b - 1) // (L // 2) + 1]
            if k in BY_S:
                i = BY_S.index(k)
                xh, pv = T.xh[:, 512 * i:512 * i + n], ("b2", "b1")[i]
            if nm[0] == "x":
                act(xh, recw.indirect(T.cand[:, a:b]), F.Copy, recn + over("cand", a, b), ["xh%d" % k])
            elif nm[0] == "w":
                mm(pv, [(T[pv][:, 0:n], T.im1[:], ar, ["im1"] + arn), (T[pv][:, 0:n], T.i1[:], xh, ["i1", "xh%d" % k])])
            elif nm[0] == "v":
                tt(df, recw.indirect(T.cand[:, a:b]), ar, A.subtract, recn + over("cand", a, b) + arn, ["df%d" % k])
            elif k in BY_S:
                act(df, T[pv][:, 0:n], F.Abs, [pv], ["df%d" % k])
            else:
                act(df, df, F.Abs, ["df%d" % k], ["df%d" % k])
        elif nm[0] == "d" and len(nm) == 2:
            rd = ["bm"] + ["df%d" % k for k in range(len(CUT) - 1) if CUT[k] < b and CUT[k + 1] > a]
            d = bank[nm]
            mm(d, [(T[d][:, a:b], T.bm[:, 15 - i:143 - i], T.df[:, 16 * a + i:16 * b:16], rd) for i in range(16)])
        elif nm == "krow":
            act(T.krow[:], T.jf[:, 0:V].indirect(kl), F.Identity, ["jfa", "jfb"] + kbn, ["krow"], bias=float(SP))
        elif nm == "keyh":
            ts(T.keyh[:], kl, float(SP - 1024), None, A.add, None, kbn, ["keyh"])
        elif nm == "keyf":
            ts(T.keyf[:, 0:12], kl, float(SP), None, A.add, None, kbn, ["keyf"])
        elif nm[:2] == "ne":
            p = int(z)
            for k, (s, n) in enumerate(SEG):
                ts(T.ne[:, p, s:s + n], T.krow[:, CL * (p + 1) - n:CL * (p + 1)], T.keyf[:, NC * p + k:NC * p + k + 1],
                   None, A.not_equal, None, ["keyf", "krow", "ne"], ["ne%d%d" % (p, k)])
        elif nm == "pl":
            if not fresh:
                mm("b6", [(T.b6[:, 32:44], T.i16[:], T.keyh[:], ["i16", "keyh"])]
                   + [(T.b6[:, 32:44], T.bo[:, 15 - u:143 - u], T.mkb[:, t, :, u:CL:16], ["bo", mkn])
                      for u in range(16)])
            if t == 1:
                dma("y", "lex2", ["keyh"] if fresh else [mkn], ["recf"], T.recs[:, R + V:2 * R], T.rec[:, V:R])
        elif nm == "o1":
            if not fresh:
                ts(T.o2[:, 16 * t:16 * t + 12], T.b6[:, 32:44], 1024.0 - SP, None, A.add, None, ["b6"], ["ob%d" % t])
        elif nm == "r1":
            if fresh:
                act(T.r1[:], tabw.indirect(kl), F.Identity, ["tab", "tab0"] + kbn, ["r1"], bias=MAGIC)
            else:
                act(T.r1[:], T.tab[:, SP:SP + 2 * V].indirect(T.o2[:, 16 * t:16 * t + 12]), F.Identity,
                    ["tab", "ch0", "ch1", "ob%d" % t], ["r1"], bias=MAGIC)
        elif nm == "cv":
            if fresh:
                ts(T.c1[:], tabw.indirect(kl), MAGIC, -MAGIC, A.add, A.add, ["tab", "tab0"] + kbn, ["c1"])
            else:
                ts(T.c1[:], T.tab[:, SP:SP + 2 * V].indirect(T.o2[:, 16 * t:16 * t + 12]), MAGIC, -MAGIC, A.add, A.add,
                   ["tab", "ch0", "ob%d" % t], ["c1"])
        elif nm == "c1":
            act(T.c1[:], T.r1[:], F.Identity, ["r1"], ["c1"], bias=-MAGIC)
        elif nm == "wf":
            ts(T.wf[:], T.cand[:], 4095.5, None, A.is_gt, None, over("cand", 0, L), ["wf"])
        elif nm == "py":
            mm("b7", [(T.b7[:, 256:256 + L], T.i16[:], T.tags[:, L * t:L * t + L], ["i16", "tag%d" % t]),
                      (T.b7[:, 256:256 + L], T.im4[:], T.wf[:], ["im4", "wf"])]
               + ([] if fresh else [(T.b7[:, 256:256 + L], T.i4[:], mk, ["i4", mkn])]))
        elif nm == "yv":
            tt(T.yv[:], T.b7[:, 256:256 + L], T.c1[:], A.add, ["b7", "c1"], ["yv"])
        elif nm[:2] == "dm":
            ts(T.dm[:, sl], T[bank["d" + z]][:, sl], -2048.0, None, A.add, None, [bank["d" + z]], [nm])
        elif nm[:2] == "fl":
            ts(T.fl[:, pa:pb], T[bank["d" + z]][:, sl], c(TH), 1.0 / 32, A.is_gt, A.subtract,
               [bank["d" + z], "th"], [nm])
        elif nm[:2] == "qb":
            act(T.qb[:, sl], T[bank["d" + z]][:, sl], F.Identity, [bank["d" + z]], [nm], scale=37.0 / 2048,
                bias=155.0 - 1022.5 / 2048)
        elif nm[:2] in ("pc", "pu") or nm[:3] == "pre":
            pc, pu, n = T[bank["c" + z]], T[bank["u" + z]][:, sl], pb - pa
            nes = ["ne%d%d" % (p, k) for p in range(pa, pb) for k in range(NC)] + ["nd%d" % k for k in range(NC)]
            early = {"c": [(pc[:, 0:n, 0:SL], T.i64[:], T.ne[:, pa:pb], ["i64"] + nes)]
                     + [(pc[:, 0:n, s + m], T.i16[:], T.keyh[:, pa:pb, k], ["i16", "keyh"])
                        for k, (s, m) in enumerate(SEG)], "u": []}
            if not fresh:
                early["c"] += [(pc[:, 0:n, s:s + m], T.in2[:], T.mkb[:, t, pa:pb, CL - m:CL], ["in2", mkn])
                               for s, m in SEG]
                early["u"] += [(pu, T.im8[:], T.mkb[:, t, pa:pb], ["im8", mkn])]
            late = {"c": [(pc[:, 0:n, s:s + m], T.on2[:], T.fl[:, pa:pb, CL - m:CL], ["on2", "fl" + z]) for s, m in SEG],
                    "u": [(pu, T.lz[:], T.fl[:, pa:pb], ["lz", "fl" + z]),
                          (pu, T.i37[:], T.dm[:, sl], ["i37"] + over("dm", a, b)),
                          (pu, T.im2[:], T.qb[:, sl], ["im2", "qb" + z])]}
            if nm[:3] == "pre":
                for k in "cu":
                    mm(bank[k + z], early[k], True, False)
            elif "pre" + z in ORDER.split():
                mm(bank[nm[1:]], late[nm[1]], not early[nm[1]], True)
            else:
                mm(bank[nm[1:]], early[nm[1]] + late[nm[1]])
        elif nm[:2] == "ef":
            act(T.ef[:, sl], T[bank["u" + z]][:, sl], F.Relu, [bank["u" + z], "eb"], [nm], bias=c(EB))
        elif nm[:2] == "rr":
            for p in range(pa, pb):
                op("v", ["dpat", bank["c" + z]], ["rr%d" % p],
                   lambda e: e.tensor_tensor_scan(T.rr[:, SL * p:SL * p + SL], T.dpat[:],
                                                  T[bank["c" + z]][:, p - pa, 0:SL], 0.0, A.mult, A.min))
        elif nm[:3] == "off":
            o = 16 * (z == "Z")
            ts(T.off[:, o:o + 16], T.rr[:, 0:L // CL * SL].indirect(T.ends[:, 0:1]), -1.0, None, A.mult, None,
               ["rr%d" % p for p in range(L // CL)] + ["ends"], [nm])
        elif nm[:2] == "sc":
            p = int(z)
            y = "A" if CL * p < PART["Z"][0] else "Z"
            o = 16 * (y == "Z") + NC * p
            tt(T.tab[:, 0:SP + V].indirect(T.off[:, o:o + NC]), T.yv[:, CL * p:CL * p + CL],
               T.ef[:, CL * p:CL * p + CL], A.add, ["off" + y, "yv", "ef" + y],
               ["tab", "spare"] + (["tab0"] if t == 0 else []))
        elif nm[:2] == "fw":
            if 0 < t < NR - 1:
                forward(home, "ab".index(z), ["r%s%d" % (z, home)])
        elif not hand_on:
            pass
        elif nm[:2] == "pr":
            pk = T[bank["k" + z]][:, 64 + a:64 + b]
            mm(bank["k" + z], [(pk, T.i64[:], T.kmask[:, sl], ["i64", "kmask"]),
                               (pk, T.i16[:], T.half[:, sl], ["i16", "half"]),
                               (pk, T.bwr[:], T.dm[:, sl], ["bwr", "dm" + z])])
        elif nm[:2] == "ks":
            op("v", ["kpat", bank["k" + z]], [nm],
               lambda e: e.tensor_tensor_scan(T.kx[:, sl], T.kpat[:, sl], T[bank["k" + z]][:, 64 + a:64 + b], 0.0,
                                              A.add, A.min))
        elif nm[:2] == "kr" and "ks" + z in ORDER.split():
            ts(T.kr[:, ca:cb], T.kx[:, a + 15:b:16], MAGIC * V, -MAGIC * V, A.add, A.add, ["ks" + z], [nm])
        elif nm[:2] == "kf" and "ks" + z in ORDER.split():
            tt(T.kf[:, ca:cb], T.kx[:, a + 15:b:16], T.kr[:, ca:cb], A.subtract, ["ks" + z, "kr" + z], [nm])
        elif nm[:2] == "pk":
            pk = T[bank[nm[1:]]][:, ca:cb]
            mm(bank[nm[1:]], [(pk, T.i16[:], T.half[:, ca:cb], ["i16", "half"])]
               + [(pk, T.bw[:, 15 - u:143 - u], T.dm[:, a + u:b:16], ["bw", "dm" + z]) for u in range(16)])
        elif nm[:2] == "kr":
            ts(T.kr[:, ca:cb], T[bank["k" + z]][:, ca:cb], MAGIC * V, -MAGIC * V, A.add, A.add, [bank["k" + z]], [nm])
        elif nm[:2] == "kf":
            tt(T.kf[:, ca:cb], T[bank["k" + z]][:, ca:cb], T.kr[:, ca:cb], A.subtract, [bank["k" + z], "kr" + z], [nm])
        elif nm[:2] == "ko":
            o = T.ko[:, 16 * t + ca:16 * t + cb]
            ts(o, T.kf[:, ca:cb], 1023.5, None, A.add, None, ["kf" + z], ["o%s%d" % (z, t)])
            if not last:
                send(nxt, "k%s%d" % (z, t + 1), ["o%s%d" % (z, t)], T.kb[:, 32 * (t + 1) + ca:32 * (t + 1) + cb], o)
        elif nm[:2] == "va":
            v = T.b0[:, 256 + a:256 + b]
            mm("b0", ([] if fresh else [(v, T.im8[:], T.mkb[:, t, pa:pb], ["im8", mkn])])
               + [(v, T.i32[:], T.yv[:, sl], ["i32", "yv"]), (v, T.i32[:], T.ef[:, sl], ["i32", "ef" + z])])
        elif nm[:2] == "vb":
            act(T.val[:, sl], T.b0[:, 256 + a:256 + b], F.Copy, ["b0"], [nm])
        elif nm == "wn":
            if LIST:
                tt(T.wn[:], tabw.indirect(kl), T.val[:], A.is_equal, ["tab", "vbA", "vbZ"] + kbn, ["wn"])
            else:
                tt(T.wn[:], tabw.indirect(kl), T.yv[:], A.is_equal, ["tab", "yv"] + kbn, ["wn"])
        elif nm in ("poE", "poL"):
            po = T.b6[:, 32:44]
            if nm == "poL" and not last:
                mm("b6", [(po, T.bo[:, 15 - u:143 - u], T.wn[:, u:L:16], ["bo", "wn"]) for u in range(16)], False, True)
            elif not last:
                mm("b6", [(po, T.i32[:], T.kf[:], ["i32"] + over("kf", 0, L))]
                   + [(po, T.bo[:, 15 - u:143 - u], T.mkb[:, t, :, u:CL:16], ["bo", mkn])
                      for u in range(0 if fresh else 16)], True, False)
        elif nm == "o2":
            o = T.o2o[:, 16 * t:16 * t + 12]
            ts(o, T.b6[:, 32:44], 1023.5, None, A.add, None, ["b6"], ["oo%d" % t])
            send(nxt, "oa%d" % (t + 1), ["oo%d" % t], T.o2[:, 16 * (t + 1):16 * (t + 1) + 12], o)
        elif nm == "pm":
            mm("b5", ([] if fresh else [(T.b5[:, 256:256 + L], T.i1[:], mk, ["i1", mkn])])
               + [(T.b5[:, 256:256 + L], T.ones[:], T.wn[:], ["ones", "wn"])])
        elif nm == "mo":
            act(mo, T.b5[:, 256:256 + L], F.Sign, ["b5"], ["mo%d" % t])
            if not last:
                send(nxt, "ma%d" % (t + 1), ["mo%d" % t], T.mkb[:, t + 1], mo)
        else:
            raise ValueError(nm)

    for t in range(NT):
        names = ORDER.split()
        if t == 0:
            early = EARLY.split()
            names = early + [nm for nm in names if nm not in early]
        for nm in names:
            if nm[0] != "<":
                step(nm, t)
            elif t > 0:
                step(nm[1:], t - 1)

    t = NT - 1
    banks = ["b1", "b2", "b6", "b7", "b1"]
    cut = [0, 192, 704, 1216, 1728, 2048]

    by_s = (2, 4)
    act(T.one[:], T.jf[:, 0:512], F.Identity, ["jfa", "jfb"], ["one"], scale=0.0, bias=1.0)
    act(T.imm[:], T.i1[:], F.Identity, ["i1"], ["imm"], scale=-MAGIC)

    def sign(k):
        a, b = cut[k], cut[k + 1]
        o = T[banks[k]][:, 0:b - a]
        act(T.so[:, a:b], T.tab[:, SP + a:SP + b], F.Sign, ["tab"], ["so%d" % k], bias=-4095.5)
        less = []
        if k in by_s:
            act(T.ro[:, a:b], T.tab[:, SP + a:SP + b], F.Identity, ["tab"], ["ro%d" % k], bias=MAGIC)
            less = [(o, T.imm[:], T.one[:, 0:b - a], ["imm", "one"]), (o, T.im2[:], T.one[:, 0:b - a], ["im2", "one"])]
        mm(banks[k], less + [(o, T.im2[:], T.so[:, a:b], ["im2", "so%d" % k])])

    def block(k):
        a, b = cut[k], cut[k + 1]
        ts(T.ro[:, a:b], T.tab[:, SP + a:SP + b], MAGIC, -(MAGIC + 2048.0), A.add, A.add, ["tab"], ["ro%d" % k])

    def store(k):
        a, b = cut[k], cut[k + 1]
        tt(T.oc[:, a:b], T[banks[k]][:, 0:b - a], T.ro[:, a:b], A.add, [banks[k], "ro%d" % k], ["oc%d" % k])
        dma("y", "stored", ["oc%d" % k], [], T.yc[:, a:b], T.oc[:, a:b])
    sign(0)
    sign(1)
    block(0)
    block(1)
    store(0)
    step("wn", t)
    sign(2)
    step("pm", t)
    sign(3)
    store(1)
    block(3)
    store(2)
    step("mo", t)
    sign(4)
    act(T.r1[:], T.jf[:, 0:V].indirect(T.ko[:, 16 * t:16 * t + 12]), F.Identity,
        ["jfa", "jfb"] + ["o%s%d" % (z, t) for z in KEYS], ["r1"])
    act(T.qb[:], T.mko[:, L * t:L * t + L].indirect(T.rv[:]), F.Copy, ["mo%d" % t, "rv"], ["qbA", "qbZ"])
    store(3)
    store(4)
    cp(T.c1[:], T.r1[:, 0:L].indirect(T.rv[:]), ["r1", "rv"], ["c1"])
    mm("b0", [(T.b0[0:8, 0:L], T.s8b[:], T.qb[:], ["s8b", "qbA"]), (T.b0[0:8, 0:L], T.s8f[:], T.c1[:], ["s8f", "c1"])])
    act(T.yks[0:8, :], T.b0[0:8, 0:L], F.Copy, ["b0"], ["yks"])
    dma("s", "stored", ["yks"], [], T.yk[:], T.yks[0:8, :])
    for sem, n in count.items():
        g.wait_ge(T.sem[sem], n)
